import numpy as np, ml_dtypes
CORES = [36,164,52,180,100,228,116,244]
N = 8
BF = ml_dtypes.bfloat16
def gentries(a):
    return np.ascontiguousarray(a.reshape(8, 16, -1).transpose(0, 2, 1)).reshape(8, -1)
def gtable(e):
    e = np.asarray(e); return np.ascontiguousarray(e.reshape(8, -1, 16).transpose(0, 2, 1)).reshape(128, -1).astype(np.int32)
S, A, DB, RO, MX = 1536, 3, 4, 3, 15
U = 128 >> DB
def parts(rng):
    nx = rng.integers(0, S, (N, 8, A, S))
    nx[:, 1::3] = (np.arange(S) + rng.integers(1, S // 8, nx[:, 1::3].shape)) % S
    lev = rng.random((N, 8, 16, 1), dtype=np.float32) * np.float32(0.75) + np.float32(0.25)
    rw = np.minimum(np.floor(rng.random((N, 8, 16, A * S), dtype=np.float32) * lev * np.float32(MX + 1)), np.float32(MX))
    cap = rng.integers(MX + 1, 129, (N, 8, 16, 1)); act = rng.integers(0, A, (N, 8, S))
    return nx, rw, cap, act
def pack(nx, rw, cap, act):
    return {"nx": np.stack([gtable(a.reshape(8, -1)) for a in nx]), "rw": np.ascontiguousarray(rw).reshape(N, 128, A * S).astype(np.float32).astype(BF),
            "cap": np.ascontiguousarray(cap).reshape(N, 128, 1).astype(np.float32), "act0": np.stack([gtable(a) for a in act])}
def stage(rng, nx, rw, cap, g, to, rew):
    cap[:, g] = 128
    for p in range(N):
        z, e, f = [int(v) for v in rng.permutation(S)[:3]]
        nx[p, g] = np.array([z, e, f])[to[p]]
        nx[p, g, :, z] = z; nx[p, g, :, e] = f; nx[p, g, :, f] = f
        rew[p, :, :, z] = 0; rew[p, :, :, e] = 0; rew[p, :, :, f] = U
    rw[:, g] = rew.reshape(N, 16, A * S)
def swing(rng):
    to = np.where(rng.random(S) < 0.4, 2 * rng.integers(0, 2, (1, A, S)), rng.integers(0, 3, (N, A, S)))
    rew = rng.integers(0, MX + 1, (N, 16, A, S)) * (rng.random(S) < 0.5)
    return to, rew
def brim(rng):
    to = 1 + (rng.random((N, A, S)) < 0.3).astype(np.int64)
    short = rng.random((N, 16, A, S)) * (16 * N) < 1
    return to, np.where(short, U - 1, rng.integers(U, MX + 1, short.shape))
def tug(rng):
    h = N // 2; o = rng.permutation(N); p, q = o[:h], o[h:2 * h]
    low = rng.integers(0, U + 1, (h, 16, A, S)) * (rng.random(S) < 0.7)
    high = U - low.reshape(16 * h, A, S)[rng.permutation(16 * h)].reshape(low.shape)
    b = rng.random((h, A, S)) < 0.5
    to = np.zeros((N, A, S), np.int64); rew = np.zeros((N, 16, A, S), np.int64)
    to[p] = np.where(b, 1, 0); to[q] = np.where(b, 0, 1)
    rew[p] = np.where(b[:, None], high, low); rew[q] = np.where(b[:, None], low, high)
    x = rng.random(rew.shape) * (16 * N)
    rew = rew + (x < 0.5).astype(np.int64) - (x > 16 * N - 0.5).astype(np.int64)
    return to, np.minimum(np.maximum(rew, 0), MX)
def setup_inputs(rng):
    return pack(*parts(rng))
def setup_inputs_ties(rng):
    nx, rw, cap, act = parts(rng); w = rw.reshape(N, 8, 16, A, S)
    nx[:, 0::4, 1:] = nx[:, 0::4, :1]; w[:, 0::4, :, 1:] = w[:, 0::4, :, :1]
    for g in (1, 5):
        m = rng.random(S) < 0.5
        nx[:, g] = np.where(m, nx[:, g, :1], nx[:, g]); w[:, g] = np.where(m, w[:, g, :, :1], w[:, g])
    for g in (2, 6):
        nx[:, g, 1:] = nx[:, g, :1]; cap[:, g] = 128
        w[:, g] = (4 * (rng.random((N, 16, 1, S)) < 0.3)).astype(np.float32)
        q = int(rng.integers(0, N)); i = int(rng.integers(0, 16))
        w[q, g, i] = 1; w[q, g, i, A - 1] = rng.integers(0, 3, S)
    for g in (3, 7):
        w[:, g] = MX * (rng.random((N, 16, A, S)) < 0.3).astype(np.float32); cap[:, g] = MX + 1
    return pack(nx, w, cap, act)
def setup_inputs_full(rng):
    nx, rw, cap, act = parts(rng)
    v = rng.integers(1, MX + 1, (N, 8, 16, 1))
    rw = np.where(rng.random(rw.shape, dtype=np.float32) < 0.03, rw, v.astype(np.float32))
    near = v * 2 ** DB + rng.integers(-1, 2, v.shape); ends = rng.choice(np.array([MX + 1, MX + 2, 127, 128]), v.shape)
    cap = np.minimum(np.maximum(np.where(rng.random(v.shape) < 0.6, near, ends), MX + 1), 128)
    rw[:, 0] = MX; rw[:, 1] = np.where(rng.random(rw[:, 1].shape) < 0.01, 1 + rng.integers(0, MX, rw[:, 1].shape), 0)
    return pack(nx, rw, cap, act)
def setup_inputs_chains(rng):
    nx, rw, cap, act = parts(rng); s = np.arange(S); a = np.arange(A)[:, None]
    nx[:, 0] = s; nx[:, 1] = np.minimum(s + 1 + a, S - 1); nx[:, 2] = (s - 1 - a) % S
    nx[:, 3] = rng.integers(0, S, (N, A, 1)); nx[:, 4] = np.argsort(rng.random((N, A, S)), axis=-1)
    nx[:, 5] = (S - 1) * rng.integers(0, 2, (N, A, S)); nx[:, 6, ::2] = s ^ 1; nx[:, 7] = nx[:1, 7]
    act[:, 1] = 0; act[:, 2] = A - 1; act[:, 4] = act[:1, 4]
    return pack(nx, rw, cap, act)
def setup_inputs_loud(rng):
    nx, rw, cap, act = parts(rng); o = rng.permutation(N); big = np.zeros((N, 8, 1, 1), bool)
    for g in range(8): big[o[g % N], g] = True
    big[:, 2] = True
    rw = np.where(big | (rng.random(rw.shape, dtype=np.float32) < 0.01), rw, np.float32(0))
    rw[o[0], 2] = 0; rw[:, 3] = 0
    for p in range(N):
        if not big[p, 7, 0, 0]: rw[p, 7] = 0
    for g, make in ((1, swing), (5, brim), (6, tug)):
        to, rew = make(rng); stage(rng, nx, rw, cap, g, to, rew)
    return pack(nx, rw, cap, act)
def setup_inputs_spread(rng):
    nx, rw, cap, act = parts(rng)
    e = np.exp2(rng.integers(-2, 3, (N, 8, 16, 1)) + rng.integers(-2, 3, (N, 8, 1, A * S))).astype(np.float32)
    rw = np.minimum(np.floor(np.float32(MX + 1) * rng.random(rw.shape, dtype=np.float32) ** e), np.float32(MX))
    nx = np.minimum(np.floor(S * rng.random(nx.shape) ** np.exp2(rng.integers(-2, 3, (N, 8, 1, 1)))).astype(np.int64), S - 1)
    cap = np.minimum(np.floor((MX + 1) * np.exp2(rng.random(cap.shape) * np.log2(128 / (MX + 1)) * 1.02)).astype(np.int64), 128)
    act = np.minimum(np.floor(A * rng.random(act.shape) ** 3).astype(np.int64), A - 1)
    return pack(nx, rw, cap, act)
def check_inputs(d):
    bad = []
    for k, lo, hi in (("nx", 0, S - 1), ("rw", 0, MX), ("cap", MX + 1, 128), ("act0", 0, A - 1)):
        v = np.asarray(d[k]).astype(np.float32)
        if not np.all((v >= lo) & (v <= hi) & (v == np.floor(v))): bad.append("range of " + k)
    return bad
def reference(nx, rw, cap, act0):
    n = np.stack([gentries(a) for a in nx]).astype(np.int64).reshape(N, 8, A, S)
    w = rw.astype(np.float32).astype(np.int32).reshape(N, 8, 16, A, S); c = cap.astype(np.int32).reshape(N, 8, 16, 1)
    act = np.stack([gentries(a) for a in act0]).astype(np.int64)
    for rnd in range(RO):
        t = np.take_along_axis(n, act[:, :, None, :], 2)[:, :, 0]
        r = np.take_along_axis(w, act[:, :, None, None, :], 3)[:, :, :, 0]
        for k in range(DB):
            r = np.minimum(r + np.take_along_axis(r, t[:, :, None, :], 3), c)
            t = np.take_along_axis(t, t, 2)
        q = np.zeros((8, A, S), np.int64)
        for p in range(N):
            for a in range(A):
                v = w[p][:, :, a] + np.take_along_axis(r[p], n[p][:, a][:, None, :], 2)
                q[:, a] += np.add.reduce(np.minimum(v, c[p]), axis=1)
        best = np.argmax(q, axis=1)
        act = np.stack([best for p in range(N)])
    return {"yr": r.reshape(N, 128, S).astype(np.float32).astype(BF), "ya": np.stack([gtable(a) for a in act]).astype(np.float32)}

@@ -1,0 +1,297 @@
+from concourse.bass import DstId, RemoteDMATransfer
+from concourse.mybir import AluOpType as A, ActivationFunctionType as F
+
+NR, ROUNDS = 8, 3
+S, NA = 1536, 3
+M = S // 16
+NV = 1152
+NS = S - NV
+MV, MS = NV // 16, NS // 16
+TV = (0, 256, 256)
+TF = (768, 896, 896)
+RS = 1152
+RC = (1024, 1024, RS)
+
+_B, _H, _F = "bfloat16", "float16", "float32"
+SCRATCH = {
+    "nxi": ("sbuf", [128, 288], "int32"), "acti": ("sbuf", [128, 96], "int32"), "capf": ("sbuf", [128, 1], _F),
+    "rwb": ("sbuf", [128, 4608], _B), "db": ("sbuf", [128, 3 * NV], _B), "xd": ("sbuf", [128, 4608], _B),
+    "nx16": ("sbuf", [128, 288], _H), "nxu": ("sbuf", [128, 288], "uint16"), "dn": ("sbuf", [128, 192], _H),
+    "xt": ("sbuf", [128, 576], "int32"), "xs": ("sbuf", [128, 576], "int32"), "xb": ("sbuf", [128, 576], _B),
+    "lu": ("sbuf", [128, 96], "uint16"), "tu0": ("sbuf", [128, 96], "uint16"), "tu1": ("sbuf", [128, 96], "uint16"),
+    "sti": ("sbuf", [128, 96], "int32"), "pi": ("sbuf", [128, 1], "int32"), "pm": ("sbuf", [128, 1], "int32"),
+    "pf": ("sbuf", [128, 1], _F), "st16": ("sbuf", [128, 96], _H),
+    "bb": ("sbuf", [128, 192], _H), "pr": ("sbuf", [128, 192], _H), "wm": ("sbuf", [128, 192], _F),
+    "ra": ("sbuf", [128, S], _B), "rb": ("sbuf", [128, S], _B), "ta": ("sbuf", [128, S], _B), "tb": ("sbuf", [128, S], _B),
+    "rk": ("sbuf", [128, S], _B), "zr": ("sbuf", [128, S - RS], _B),
+    "tv0": ("sbuf", [128, NV], _B), "tv1": ("sbuf", [128, NV], _B), "tv2": ("sbuf", [128, NV], _B),
+    "zs": ("sbuf", [128, 3 * NS], _B), "ts": ("sbuf", [128, 3 * NS], _B),
+    "x0": ("sbuf", [128, MV], _F), "xs0": ("sbuf", [128, MS], _F),
+    "eo": ("sbuf", [128, 2 * MV], _H), "eg": ("sbuf", [128, 192], _H),
+    "yb": ("sbuf", [128, S], _B), "yt": ("sbuf", [128, 96], _F), "yf": ("sbuf", [128, 96], _F),
+    "selx": ("sbuf", [128, 1024], _B), "pa": ("sbuf", [128, 128], _B), "pb": ("sbuf", [128, 128], _B),
+    "idb": ("sbuf", [128, 128], _B), "i1": ("sbuf", [128, 128], _B), "i2": ("sbuf", [128, 128], _B),
+    "zx": ("sbuf", [128, 144], _B), "zq": ("sbuf", [128, 144], _B), "nzq": ("sbuf", [128, 144], _B),
+}
+for _k in range(8):
+    SCRATCH["b%d" % _k] = ("psum", [128, 512], _F)
+    SCRATCH["ev%d" % _k] = ("sbuf", [128, 2 * MV], _H)
+for _r in range(ROUNDS):
+    SCRATCH["o%d" % _r] = ("sbuf", [128, 192], _H)
+    for _k in range(NR):
+        SCRATCH["v%d_%d" % (_r, _k)] = ("sbuf", [128, 192], _H)
+SEMAPHORES = ["cV", "cS", "cP", "cG", "lnx", "lact", "lcap", "lrw0", "lrw1", "lrw2", "st0", "st1", "loc"]
+SEMAPHORES += ["ae%d" % k for k in range(NR)] + ["a%d_%d" % (r, k) for r in range(ROUNDS) for k in range(NR)]
+
+
+def rank_program(g, core, T, topo):
+    rank = T.rank_of(core)
+    if rank is None:
+        return
+    queue = {"V": g.vector, "S": g.scalar, "P": g.tensor, "G": g, "Y": g.sync}
+    V, SC, PE = g.vector, g.scalar, g.tensor
+    count = {"V": 0, "S": 0, "P": 0, "G": 0}
+    seen = {}
+
+    def wait(q, *toks):
+        for name, val in toks:
+            if seen.get((q, name), 0) < val:
+                queue[q].wait_ge(T.sem[name], val)
+                seen[(q, name)] = val
+
+    def mark(q, ins):
+        count[q] += 1
+        ins.then_inc(T.sem["c" + q], 1)
+        return ("c" + q, count[q])
+
+    def load(q, name, out, in_):
+        queue[q].dma_start(out, in_).then_inc(T.sem[name], 16)
+        return (name, 16)
+
+    def copy(deps, out, in_):
+        wait("V", *deps)
+        return mark("V", V.tensor_copy(out, in_))
+
+    def tt(deps, out, a, b, op):
+        wait("V", *deps)
+        return mark("V", V.tensor_tensor(out, a, b, op))
+
+    def tsc(deps, out, a, s1, s2, op0, op1=None):
+        wait("V", *deps)
+        if op1 is None:
+            return mark("V", V.tensor_scalar(out, a, s1, None, op0))
+        return mark("V", V.tensor_scalar(out, a, s1, s2, op0, op1))
+
+    def act(deps, out, in_, func=F.Copy, *more):
+        wait("S", *deps)
+        return mark("S", SC.activation(out, in_, func, *more))
+
+    def mm(deps, out, lhsT, rhs, start, stop):
+        wait("P", *deps)
+        ins = PE.matmul(out, lhsT, rhs, start, stop)
+        return mark("P", ins) if stop else None
+
+    def group(deps, out, pairs):
+        wait("P", *deps)
+        tok = None
+        for n, (l, r) in enumerate(pairs):
+            tok = mm([], out, l, r, n == 0, n == len(pairs) - 1)
+        return tok
+
+    def fold(deps, out, z, buf, a, b):
+        return group(deps, out, [(z[:, 15 - i:143 - i], buf[:, a + i:b:16]) for i in range(16)])
+
+    def select(tok, name, pattern, op, fill, base, cm):
+        wait("G", tok)
+        return mark("G", g.affine_select(T[name][:], T[name][:], pattern, op, fill, base, cm))
+
+    tnx = load("Y", "lnx", T.nxi[:], T.nx[:])
+    tact = load("S", "lact", T.acti[:], T.act0[:])
+    tcap = load("S", "lcap", T.capf[:], T.cap[:])
+    trw = [load("Y", "lrw%d" % a, T.rwb[:, a * S:(a + 1) * S], T.rw[:, a * S:(a + 1) * S]) for a in range(NA)]
+
+    zero = {}
+    for n in ("pa", "pb", "selx", "idb", "zx", "eg"):
+        zero[n] = mark("V", V.memset(T[n][:], 0.0))
+    zero["zq"] = mark("V", V.memset(T.zq[:], 1.0))
+    pp = [[-16, 8], [1000, 2], [-1, 8]]
+    k = select(zero["pa"], "pa", pp, A.not_equal, 256.0, 0, 1)
+    kpa = select(k, "pa", pp, A.not_equal, 1.0, -1000, 1)
+    k = select(zero["pb"], "pb", pp, A.not_equal, 256.0, -8, 1)
+    kpb = select(k, "pb", pp, A.not_equal, 1.0, -1008, 1)
+    ksx = select(zero["selx"], "selx", [[-1, 8], [-8, 16], [0, 8]], A.not_equal, 1.0, 0, 1)
+    kid = select(zero["idb"], "idb", [[-1, 128]], A.not_equal, 1.0, 0, 1)
+    ksti = mark("G", g.iota(T.sti[:], [[16, 96]], 0, 0))
+    kpi = mark("G", g.iota(T.pi[:], [[1, 1]], 0, 1))
+    k = select(zero["zx"], "zx", [[-16, 9], [1000, 16]], A.not_equal, 1.0, -15000, 1)
+    kzx = select(k, "zx", [[-16, 9], [1000, 16]], A.not_equal, 256.0, -15008, 1)
+    k = select(zero["zq"], "zq", [[0, 9], [1, 16]], A.is_ge, 0.0, -15, 0)
+    k = select(k, "zq", [[-16, 9], [0, 16]], A.is_ge, 0.0, 0, 1)
+    kzq = select(k, "zq", [[16, 9], [0, 16]], A.is_ge, 0.0, 15, -1)
+
+    t16 = copy([tnx], T.nx16[:], T.nxi[:])
+    pA = group([t16, kpa], T.b1[:, 0:288], [(T.pa[:], T.nx16[:])])
+    pB = group([kpb], T.b2[:, 0:288], [(T.pb[:], T.nx16[:])])
+    b1t = tsc([tact], T.bb[:, 0:96], T.acti[:], 1.0, None, A.is_equal)
+    b2t = tsc([], T.bb[:, 96:192], T.acti[:], 2.0, None, A.is_equal)
+
+    def digits(p, bank, lo):
+        c = slice(lo, lo + 288)
+        a = copy([p], T.xt[:, c], bank[:, 0:288])
+        b = tsc([a], T.xs[:, c], T.xt[:, c], 8, 255, A.logical_shift_right, A.bitwise_and)
+        return copy([b], T.xb[:, c], T.xs[:, c])
+
+    dig = [digits(pA, T.b1, 0), digits(pB, T.b2, 288)]
+    kdn = [tt([t16], T.dn[:, 96 * a:96 * a + 96], T.nx16[:, 96 * a + 96:96 * a + 192], T.nx16[:, 0:96], A.subtract)
+           for a in range(2)]
+    ki1 = tsc([kid], T.i1[:], T.idb[:], 1536.0, None, A.mult)
+    ki2 = tsc([], T.i2[:], T.idb[:], 3072.0, None, A.mult)
+    kpm = tsc([kpi], T.pm[:], T.pi[:], 15, None, A.bitwise_and)
+    kpf = copy([kpm], T.pf[:], T.pm[:])
+    kst = tsc([kpf, ksti], T.st16[:], T.sti[:], T.pf[:], None, A.add)
+    kn0 = copy([], T.nxu[:], T.nxi[:])
+    bank_free = {}
+    xdt = []
+    for n in range(16):
+        h, j = n // 8, n % 8
+        b = 3 + n % 5
+        src = T["b%d" % b][:, 0:288]
+        tok = group([ksx, dig[h]] + bank_free.get(b, []), src,
+                    [(T.selx[:, 128 * j:128 * j + 128], T.xb[:, 288 * h:288 * h + 288])])
+        out = T.xd[:, j + 8 * h::16]
+        if h == 0 or j % 2 == 1:
+            bank_free[b] = [act([tok], out, src)]
+        else:
+            bank_free[b] = [copy([tok], out, src)]
+        xdt += bank_free[b]
+
+    def caps(q, a):
+        out, in_ = T.db[:, a * NV:a * NV + NV], T.rwb[:, a * S:a * S + NV]
+        wait(q, trw[a], tcap)
+        if q == "V":
+            return mark("V", V.tensor_scalar(out, in_, -1.0, T.capf[:], A.mult, A.add))
+        return mark("S", SC.activation(out, in_, F.Identity, T.capf[:], -1.0))
+
+    T_, R_, TU = [T.ta, T.tb], [T.ra, T.rb], [T.tu0, T.tu1]
+    others = [T.cores[(rank + n) % NR] for n in range(1, NR)]
+    before = [(rank - n) % NR for n in range(1, NR)]
+
+    def share(deps, src, land, sem):
+        wait("G", *deps)
+        mask = topo.mask(core, others[0])
+        ids = []
+        for d in others:
+            mask &= topo.mask(core, d)
+            rid, pid = topo.addr(d, core)
+            ids.append(DstId(rid=rid, pnc=pid))
+        g.remote_dma_fused([RemoteDMATransfer(dst_ids=ids, dma_engine_mask=mask, remote_sem=T.sem[sem], srcs=[src],
+                                              dsts=[land for d in others])], local_sem=T.sem["loc"])
+        return len([n for n in range(16) if mask >> n & 1])
+
+    sent = 0
+    tb_ = [b1t, b2t] + bank_free[5]
+    for rnd in range(ROUNDS):
+        first, last = rnd == 0, rnd == ROUNDS - 1
+        pL = group(tb_ + [ki1, ki2, kst], T.b5[:, 0:96],
+                   [(T.i1[:], T.bb[:, 0:96]), (T.i2[:], T.bb[:, 96:192]), (T.idb[:], T.st16[:])])
+        kpr = tt(tb_ + kdn, T.pr[:], T.bb[:], T.dn[:], A.mult)
+        kl = copy([pL], T.lu[:], T.b5[:, 0:96])
+        pT = group([kpr], T.b0[:, 0:96], [(T.idb[:], T.nx16[:, 0:96]), (T.idb[:], T.pr[:, 0:96]), (T.idb[:], T.pr[:, 96:192])])
+        kt = act([kl] + (xdt if first else []), T.ta[:], T.xd[:].indirect(T.lu[:]))
+        if first:
+            kd = [caps("V", 0), None, caps("V", 2)]
+        wait("V", kl, *trw)
+        kr = [copy([], T.ra[:, 0:RC[0]], T.rwb[:].indirect(T.lu[:, 0:RC[0] // 16]))]
+        ktu = copy([pT], T.tu0[:], T.b0[:, 0:96])
+        kr.append(copy([], T.ra[:, RC[0]:S], T.rwb[:].indirect(T.lu[:, RC[0] // 16:M])))
+        krk = [copy(kr, T.rk[:], T.ra[:])]
+        if first:
+            knz = tsc([kzq], T.nzq[:], T.zq[:], -1.0, None, A.mult)
+            pe = [fold([trw[a], kzq] + xdt, T["b%d" % (1 + a)][:, 0:MV], T.zq, T.rwb, a * S, a * S + NV) for a in range(NA)]
+
+        def preload():
+            for a in range(NA):
+                mm([kid], T["b%d" % (1 + a)][:, 0:NS], T.idb[:], T.rwb[:, a * S + NV:a * S + S], True, False)
+
+        if not first:
+            preload()
+        cur = 0
+        ktx = [kt]
+        for st in range(3):
+            tc, tn, rc, rn, tu, tun = T_[cur], T_[1 - cur], R_[cur], R_[1 - cur], TU[cur], TU[1 - cur]
+            tv, tf, rcut = TV[st], TF[st], RC[st]
+            hv = [copy([ktu] + ktx, tn[:, 0:tv], tc[:].indirect(tu[:, 0:tv // 16]))] if tv else []
+            h1 = act([ktu] + ktx, tn[:, tv:tf], tc[:].indirect(tu[:, tv // 16:tf // 16]))
+            h2 = act([], tn[:, tf:S], tc[:].indirect(tu[:, tf // 16:M]))
+            ktx = hv + [h2]
+            fold(hv + [h1, kzx], T.b0[:, 0:tf // 16], T.zx, tn, 0, tf)
+            px = fold([h2], T.b0[:, tf // 16:M], T.zx, tn, tf, S)
+            k1 = tt(kr + krk + [ktu], rn[:, 0:rcut], rc[:].indirect(tu[:, 0:rcut // 16]), T.rk[:, 0:rcut], A.add)
+            k2 = tt([], rn[:, rcut:S], rc[:].indirect(tu[:, rcut // 16:M]), T.rk[:, rcut:S], A.add)
+            kr = [k2]
+            krk = [act([k1], T.rk[:, 0:rcut], rn[:, 0:rcut])]
+            if st < 2:
+                krk.append(copy([k2], T.rk[:, rcut:S], rn[:, rcut:S]))
+            if first and st == 0:
+                k = copy([pe[0]], T.x0[:], T.b1[:, 0:MV])
+                tt([k, pe[1]], T.eo[:, 0:MV], T.b2[:, 0:MV], T.x0[:], A.subtract)
+                ke = tt([pe[2]], T.eo[:, MV:2 * MV], T.b3[:, 0:MV], T.x0[:], A.subtract)
+                sent += share([ke], T.eo[:], T["ev%d" % rank][:], "ae%d" % rank)
+            ktu = copy([px], tun[:], T.b0[:, 0:96])
+            cur = 1 - cur
+        rc, rn, tu = R_[cur], R_[1 - cur], TU[cur]
+        mm(kr, T.b6[:, 0:S - RS], T.idb[:], rc[:, RS:S], True, False)
+        hz = act([ktu] + kr, T.zr[:], rc[:].indirect(tu[:, RS // 16:M]))
+        pz = mm([hz], T.b6[:, 0:S - RS], T.idb[:], T.zr[:], False, True)
+        ks = act([pz], rn[:, RS:S], T.b6[:, 0:S - RS])
+        kv = tt([ktu] + kr + krk, rn[:, 0:RS], rc[:].indirect(tu[:, 0:RS // 16]), T.rk[:, 0:RS], A.add)
+        if first:
+            wait("P", ke)
+            preload()
+            kd[1] = caps("S", 1)
+        hz = [act([kv, ks, kn0], T.zs[:, a * NS:a * NS + NS], rn[:].indirect(T.nxu[:, a * M + MV:a * M + M])) for a in range(NA)]
+        pz = [mm([hz[a]], T["b%d" % (1 + a)][:, 0:NS], T.idb[:], T.zs[:, a * NS:a * NS + NS], False, True) for a in range(NA)]
+        wait("S", tcap)
+        kre = [act([pz[a]], T.ts[:, a * NS:a * NS + NS], T["b%d" % (1 + a)][:, 0:NS], F.Relu, T.capf[:], -1.0) for a in range(NA)]
+        hv = [tt([kv, ks, kd[a]], T["tv%d" % a][:], rn[:].indirect(T.nxu[:, a * M:a * M + MV]), T.db[:, a * NV:a * NV + NV], A.min)
+              for a in range(NA)]
+        pv0 = fold([hv[0], kzq], T.b4[:, 0:MV], T.zq, T.tv0, 0, NV)
+        if first:
+            pv1 = fold([hv[1]], T.b5[:, 0:MV], T.zq, T.tv1, 0, NV)
+        ps = fold([kre[2], knz], T.b7[:, 0:3 * MS], T.nzq, T.ts, 0, 3 * NS)
+        if not first:
+            pv1 = fold([hv[1]], T.b5[:, 0:MV], T.zq, T.tv1, 0, NV)
+        pv2 = fold([hv[2]], T.b6[:, 0:MV], T.zq, T.tv2, 0, NV)
+        kx0 = act([pv0], T.x0[:], T.b4[:, 0:MV])
+        kx1 = act([ps], T.xs0[:], T.b7[:, 0:MS])
+        o = T["o%d" % rnd]
+        tt([kx1], o[:, MV:M], T.b7[:, MS:2 * MS], T.xs0[:], A.subtract)
+        tt([], o[:, M + MV:2 * M], T.b7[:, 2 * MS:3 * MS], T.xs0[:], A.subtract)
+        tt([pv1, kx0], o[:, 0:MV], T.b5[:, 0:MV], T.x0[:], A.subtract)
+        ko = tt([pv2], o[:, M:M + MV], T.b6[:, 0:MV], T.x0[:], A.subtract)
+        sent += share([ko], o[:], T["v%d_%d" % (rnd, rank)][:], "a%d_%d" % (rnd, rank))
+        if last:
+            wait("V", tcap)
+            ky = tsc([kv, ks], T.yb[:], rn[:], T.capf[:], None, A.min)
+            wait("Y", ky)
+            sy = load("Y", "st0", T.yr[:], T.yb[:])
+        if first:
+            mm([ke, ko], T.b7[:, 0:2 * MV], T.idb[:], T.eo[:], True, False)
+            for n, p in enumerate(before):
+                k = mm([("ae%d" % p, 8)], T.b7[:, 0:2 * MV], T.idb[:], T["ev%d" % p][:], False, n == NR - 2)
+            copy([k], T.eg[:, 0:MV], T.b7[:, 0:MV])
+            keg = copy([], T.eg[:, M:M + MV], T.b7[:, MV:2 * MV])
+        mm([keg, ko], T.b4[:, 0:192], T.idb[:], T.eg[:], True, False)
+        mm([], T.b4[:, 0:192], T.idb[:], o[:], False, False)
+        for n, p in enumerate(before):
+            pD = mm([("a%d_%d" % (rnd, p), 8)], T.b4[:, 0:192], T.idb[:], T["v%d_%d" % (rnd, p)][:], False, n == NR - 2)
+        tsc([pD], T.wm[:, 0:96], T.b4[:, 96:192], -1.0, 0.0, A.add, A.max)
+        kw = tsc([], T.wm[:, 96:192], T.b4[:, 0:96], 0.0, None, A.max)
+        kb = tt([kw], T.bb[:], T.b4[:, 0:192], T.wm[:], A.is_gt)
+        tb_ = [kb]
+    k = tsc([kb], T.yt[:], T.bb[:, 96:192], 2.0, None, A.mult)
+    k = tt([k], T.yf[:], T.yt[:], T.bb[:, 0:96], A.add)
+    wait("Y", k)
+    sa = load("Y", "st1", T.ya[:], T.yf[:])
+    wait("Y", sy, sa)
+    wait("G", ("loc", sent), ("cV", count["V"]), ("cS", count["S"]), ("cP", count["P"]), ("cG", count["G"]))

@@ -4,44 +4,50 @@ from concourse.mybir import AluOpType as A, ActivationFunctionType as F
 NR, ROUNDS = 8, 3
 S, NA = 1536, 3
 M = S // 16
-NV = 1152
-NS = S - NV
-MV, MS = NV // 16, NS // 16
-TV = (0, 256, 256)
-TF = (768, 896, 896)
-RS = 1152
-RC = (1024, 1024, RS)
+H = S // 2
+MA = 64
+SA = 16 * MA
+BLK = ((0, MA), (MA, M))
+XG, XS = 384, 192
+XG0 = 640
+RS = 512
+EAT = 2
+XDV = 5
 
-_B, _H, _F = "bfloat16", "float16", "float32"
+_B, _H, _F, _I, _U = "bfloat16", "float16", "float32", "int32", "uint16"
 SCRATCH = {
-    "nxi": ("sbuf", [128, 288], "int32"), "acti": ("sbuf", [128, 96], "int32"), "capf": ("sbuf", [128, 1], _F),
-    "rwb": ("sbuf", [128, 4608], _B), "db": ("sbuf", [128, 3 * NV], _B), "xd": ("sbuf", [128, 4608], _B),
-    "nx16": ("sbuf", [128, 288], _H), "nxu": ("sbuf", [128, 288], "uint16"), "dn": ("sbuf", [128, 192], _H),
-    "xt": ("sbuf", [128, 576], "int32"), "xs": ("sbuf", [128, 576], "int32"), "xb": ("sbuf", [128, 576], _B),
-    "lu": ("sbuf", [128, 96], "uint16"), "tu0": ("sbuf", [128, 96], "uint16"), "tu1": ("sbuf", [128, 96], "uint16"),
-    "sti": ("sbuf", [128, 96], "int32"), "pi": ("sbuf", [128, 1], "int32"), "pm": ("sbuf", [128, 1], "int32"),
-    "pf": ("sbuf", [128, 1], _F), "st16": ("sbuf", [128, 96], _H),
-    "bb": ("sbuf", [128, 192], _H), "pr": ("sbuf", [128, 192], _H), "wm": ("sbuf", [128, 192], _F),
-    "ra": ("sbuf", [128, S], _B), "rb": ("sbuf", [128, S], _B), "ta": ("sbuf", [128, S], _B), "tb": ("sbuf", [128, S], _B),
-    "rk": ("sbuf", [128, S], _B), "zr": ("sbuf", [128, S - RS], _B),
-    "tv0": ("sbuf", [128, NV], _B), "tv1": ("sbuf", [128, NV], _B), "tv2": ("sbuf", [128, NV], _B),
-    "zs": ("sbuf", [128, 3 * NS], _B), "ts": ("sbuf", [128, 3 * NS], _B),
-    "x0": ("sbuf", [128, MV], _F), "xs0": ("sbuf", [128, MS], _F),
-    "eo": ("sbuf", [128, 2 * MV], _H), "eg": ("sbuf", [128, 192], _H),
-    "yb": ("sbuf", [128, S], _B), "yt": ("sbuf", [128, 96], _F), "yf": ("sbuf", [128, 96], _F),
-    "selx": ("sbuf", [128, 1024], _B), "pa": ("sbuf", [128, 128], _B), "pb": ("sbuf", [128, 128], _B),
-    "idb": ("sbuf", [128, 128], _B), "i1": ("sbuf", [128, 128], _B), "i2": ("sbuf", [128, 128], _B),
-    "zx": ("sbuf", [128, 144], _B), "zq": ("sbuf", [128, 144], _B), "nzq": ("sbuf", [128, 144], _B),
+    "nxi": ("sbuf", [128, 288], _I), "acti": ("sbuf", [128, 96], _I), "capf": ("sbuf", [128, 1], _F),
+    "rwb": ("sbuf", [128, 4608], _B), "db": ("sbuf", [128, 2 * S], _B), "xd": ("sbuf", [128, 4608], _B),
+    "nx16": ("sbuf", [128, 288], _H), "nxu": ("sbuf", [128, 288], _U), "m3": ("sbuf", [128, 288], _H),
+    "prod": ("sbuf", [128, 288], _H), "act16": ("sbuf", [128, 96], _B),
+    "xt": ("sbuf", [128, 576], _I), "xs": ("sbuf", [128, 576], _I), "xb": ("sbuf", [128, 576], _B),
+    "yt": ("sbuf", [128, 192], _I), "ys": ("sbuf", [128, 192], _I), "yd": ("sbuf", [128, 192], _B),
+    "lu": ("sbuf", [128, 96], _U), "sti": ("sbuf", [128, 96], _I), "pi": ("sbuf", [128, 1], _I), "pm": ("sbuf", [128, 1], _I),
+    "pf": ("sbuf", [128, 1], _F), "st16": ("sbuf", [128, 96], _H), "capb": ("sbuf", [128, 1], _B), "nsc": ("sbuf", [128, 1], _F),
+    "bb": ("sbuf", [128, 192], _H), "wm": ("sbuf", [128, 192], _F),
+    "zr": ("sbuf", [128, RS], _B), "tv0": ("sbuf", [128, S], _B), "tv1": ("sbuf", [128, S], _B),
+    "zs": ("sbuf", [128, S], _B), "ts": ("sbuf", [128, S], _B),
+    "x0": ("sbuf", [128, 192], _F), "eo": ("sbuf", [128, 192], _H),
+    "yb": ("sbuf", [128, S], _B), "yf": ("sbuf", [128, 96], _F),
+    "pa": ("sbuf", [128, 128], _B), "pb": ("sbuf", [128, 128], _B), "idz": ("sbuf", [128, 136], _B), "i1": ("sbuf", [128, 128], _B),
+    "zx": ("sbuf", [128, 144], _B), "zq": ("sbuf", [128, 144], _B),
 }
+for _k in range(5):
+    SCRATCH["r%d" % _k] = ("sbuf", [128, S], _B)
+for _k in range(4):
+    SCRATCH["k%d" % _k] = ("sbuf", [128, S], _B)
+    SCRATCH["t%d" % _k] = ("sbuf", [128, S], _B)
+    SCRATCH["u%d" % _k] = ("sbuf", [128, 96], _U)
 for _k in range(8):
     SCRATCH["b%d" % _k] = ("psum", [128, 512], _F)
-    SCRATCH["ev%d" % _k] = ("sbuf", [128, 2 * MV], _H)
+    SCRATCH["ev%d" % _k] = ("sbuf", [128, 192], _H)
 for _r in range(ROUNDS):
     SCRATCH["o%d" % _r] = ("sbuf", [128, 192], _H)
     for _k in range(NR):
         SCRATCH["v%d_%d" % (_r, _k)] = ("sbuf", [128, 192], _H)
 SEMAPHORES = ["cV", "cS", "cP", "cG", "lnx", "lact", "lcap", "lrw0", "lrw1", "lrw2", "st0", "st1", "loc"]
-SEMAPHORES += ["ae%d" % k for k in range(NR)] + ["a%d_%d" % (r, k) for r in range(ROUNDS) for k in range(NR)]
+SEMAPHORES += ["ae%d" % k for k in range(NR)]
+SEMAPHORES += ["a%d_%d_%d" % (r, x, k) for r in range(ROUNDS) for x in range(2) for k in range(NR)]
 
 
 def rank_program(g, core, T, topo):
@@ -52,6 +58,9 @@ def rank_program(g, core, T, topo):
     V, SC, PE = g.vector, g.scalar, g.tensor
     count = {"V": 0, "S": 0, "P": 0, "G": 0}
     seen = {}
+    B = [T["b%d" % n] for n in range(8)]
+    R, K, TD, U = ([T["%s%d" % (c, n)] for n in range(k)] for c, k in (("r", 5), ("k", 4), ("t", 4), ("u", 4)))
+    idb = T.idz[:, 0:128]
 
     def wait(q, *toks):
         for name, val in toks:
@@ -101,80 +110,28 @@ def rank_program(g, core, T, topo):
     def fold(deps, out, z, buf, a, b):
         return group(deps, out, [(z[:, 15 - i:143 - i], buf[:, a + i:b:16]) for i in range(16)])
 
-    def select(tok, name, pattern, op, fill, base, cm):
+    def pick(tok, name, pattern, op, fill, base, cm):
         wait("G", tok)
         return mark("G", g.affine_select(T[name][:], T[name][:], pattern, op, fill, base, cm))
 
-    tnx = load("Y", "lnx", T.nxi[:], T.nx[:])
-    tact = load("S", "lact", T.acti[:], T.act0[:])
-    tcap = load("S", "lcap", T.capf[:], T.cap[:])
-    trw = [load("Y", "lrw%d" % a, T.rwb[:, a * S:(a + 1) * S], T.rw[:, a * S:(a + 1) * S]) for a in range(NA)]
-
-    zero = {}
-    for n in ("pa", "pb", "selx", "idb", "zx", "eg"):
-        zero[n] = mark("V", V.memset(T[n][:], 0.0))
-    zero["zq"] = mark("V", V.memset(T.zq[:], 1.0))
-    pp = [[-16, 8], [1000, 2], [-1, 8]]
-    k = select(zero["pa"], "pa", pp, A.not_equal, 256.0, 0, 1)
-    kpa = select(k, "pa", pp, A.not_equal, 1.0, -1000, 1)
-    k = select(zero["pb"], "pb", pp, A.not_equal, 256.0, -8, 1)
-    kpb = select(k, "pb", pp, A.not_equal, 1.0, -1008, 1)
-    ksx = select(zero["selx"], "selx", [[-1, 8], [-8, 16], [0, 8]], A.not_equal, 1.0, 0, 1)
-    kid = select(zero["idb"], "idb", [[-1, 128]], A.not_equal, 1.0, 0, 1)
-    ksti = mark("G", g.iota(T.sti[:], [[16, 96]], 0, 0))
-    kpi = mark("G", g.iota(T.pi[:], [[1, 1]], 0, 1))
-    k = select(zero["zx"], "zx", [[-16, 9], [1000, 16]], A.not_equal, 1.0, -15000, 1)
-    kzx = select(k, "zx", [[-16, 9], [1000, 16]], A.not_equal, 256.0, -15008, 1)
-    k = select(zero["zq"], "zq", [[0, 9], [1, 16]], A.is_ge, 0.0, -15, 0)
-    k = select(k, "zq", [[-16, 9], [0, 16]], A.is_ge, 0.0, 0, 1)
-    kzq = select(k, "zq", [[16, 9], [0, 16]], A.is_ge, 0.0, 15, -1)
-
-    t16 = copy([tnx], T.nx16[:], T.nxi[:])
-    pA = group([t16, kpa], T.b1[:, 0:288], [(T.pa[:], T.nx16[:])])
-    pB = group([kpb], T.b2[:, 0:288], [(T.pb[:], T.nx16[:])])
-    b1t = tsc([tact], T.bb[:, 0:96], T.acti[:], 1.0, None, A.is_equal)
-    b2t = tsc([], T.bb[:, 96:192], T.acti[:], 2.0, None, A.is_equal)
-
-    def digits(p, bank, lo):
-        c = slice(lo, lo + 288)
-        a = copy([p], T.xt[:, c], bank[:, 0:288])
-        b = tsc([a], T.xs[:, c], T.xt[:, c], 8, 255, A.logical_shift_right, A.bitwise_and)
-        return copy([b], T.xb[:, c], T.xs[:, c])
-
-    dig = [digits(pA, T.b1, 0), digits(pB, T.b2, 288)]
-    kdn = [tt([t16], T.dn[:, 96 * a:96 * a + 96], T.nx16[:, 96 * a + 96:96 * a + 192], T.nx16[:, 0:96], A.subtract)
-           for a in range(2)]
-    ki1 = tsc([kid], T.i1[:], T.idb[:], 1536.0, None, A.mult)
-    ki2 = tsc([], T.i2[:], T.idb[:], 3072.0, None, A.mult)
-    kpm = tsc([kpi], T.pm[:], T.pi[:], 15, None, A.bitwise_and)
-    kpf = copy([kpm], T.pf[:], T.pm[:])
-    kst = tsc([kpf, ksti], T.st16[:], T.sti[:], T.pf[:], None, A.add)
-    kn0 = copy([], T.nxu[:], T.nxi[:])
-    bank_free = {}
-    xdt = []
-    for n in range(16):
-        h, j = n // 8, n % 8
-        b = 3 + n % 5
-        src = T["b%d" % b][:, 0:288]
-        tok = group([ksx, dig[h]] + bank_free.get(b, []), src,
-                    [(T.selx[:, 128 * j:128 * j + 128], T.xb[:, 288 * h:288 * h + 288])])
-        out = T.xd[:, j + 8 * h::16]
-        if h == 0 or j % 2 == 1:
-            bank_free[b] = [act([tok], out, src)]
-        else:
-            bank_free[b] = [copy([tok], out, src)]
-        xdt += bank_free[b]
-
-    def caps(q, a):
-        out, in_ = T.db[:, a * NV:a * NV + NV], T.rwb[:, a * S:a * S + NV]
-        wait(q, trw[a], tcap)
+    def dup(q, deps, k, a, b):
+        if a >= b:
+            return []
         if q == "V":
-            return mark("V", V.tensor_scalar(out, in_, -1.0, T.capf[:], A.mult, A.add))
-        return mark("S", SC.activation(out, in_, F.Identity, T.capf[:], -1.0))
+            return [copy(deps, K[k][:, a:b], R[k][:, a:b])]
+        if q == "S":
+            return [act(deps, K[k][:, a:b], R[k][:, a:b])]
+        wait("G", *deps)
+        return [mark("G", g.affine_select(K[k][:, a:b], R[k][:, a:b], [[0, b - a]], A.is_ge, 0.0, 0, 0))]
 
-    T_, R_, TU = [T.ta, T.tb], [T.ra, T.rb], [T.tu0, T.tu1]
+    def digits(deps, src, ti, si, out):
+        a = copy(deps, ti, src)
+        b = tsc([a], si, ti, 8, 255, A.logical_shift_right, A.bitwise_and)
+        return copy([b], out, si)
+
     others = [T.cores[(rank + n) % NR] for n in range(1, NR)]
     before = [(rank - n) % NR for n in range(1, NR)]
+    sent = [0]
 
     def share(deps, src, land, sem):
         wait("G", *deps)
@@ -186,112 +143,264 @@ def rank_program(g, core, T, topo):
             ids.append(DstId(rid=rid, pnc=pid))
         g.remote_dma_fused([RemoteDMATransfer(dst_ids=ids, dma_engine_mask=mask, remote_sem=T.sem[sem], srcs=[src],
                                               dsts=[land for d in others])], local_sem=T.sem["loc"])
-        return len([n for n in range(16) if mask >> n & 1])
+        sent[0] += len([n for n in range(16) if mask >> n & 1])
 
-    sent = 0
-    tb_ = [b1t, b2t] + bank_free[5]
+    arrival = len(topo.engines(others[0], core))
+
+    tnx = load("Y", "lnx", T.nxi[:], T.nx[:])
+    tact = load("S", "lact", T.acti[:], T.act0[:])
+    tcap = load("S", "lcap", T.capf[:], T.cap[:])
+    trw = [load("Y", "lrw%d" % a, T.rwb[:, a * S:(a + 1) * S], T.rw[:, a * S:(a + 1) * S]) for a in range(NA)]
+
+    zero = {}
+    for n in ("pa", "pb", "idz", "zx"):
+        zero[n] = mark("V", V.memset(T[n][:], 0.0))
+    zero["zq"] = mark("V", V.memset(T.zq[:], 1.0))
+    pp = [[-16, 8], [1000, 2], [-1, 8]]
+    k = pick(zero["pa"], "pa", pp, A.not_equal, 256.0, 0, 1)
+    kpa = pick(k, "pa", pp, A.not_equal, 1.0, -1000, 1)
+    k = pick(zero["pb"], "pb", pp, A.not_equal, 256.0, -8, 1)
+    kpb = pick(k, "pb", pp, A.not_equal, 1.0, -1008, 1)
+    kid = pick(zero["idz"], "idz", [[-1, 136]], A.not_equal, 1.0, 0, 1)
+    kpi = mark("G", g.iota(T.pi[:], [[1, 1]], 0, 1))
+    ksti = mark("G", g.iota(T.sti[:], [[16, 96]], 0, 0))
+    k = pick(zero["zx"], "zx", [[-16, 9], [1000, 16]], A.not_equal, 1.0, -15000, 1)
+    kzx = pick(k, "zx", [[-16, 9], [1000, 16]], A.not_equal, 256.0, -15008, 1)
+    k = pick(zero["zq"], "zq", [[0, 9], [1, 16]], A.is_ge, 0.0, -15, 0)
+    k = pick(k, "zq", [[-16, 9], [0, 16]], A.is_ge, 0.0, 0, 1)
+    kzq = pick(k, "zq", [[16, 9], [0, 16]], A.is_ge, 0.0, 15, -1)
+
+    for a in range(NA):
+        km = tsc([tact], T.m3[:, a * M:a * M + M], T.acti[:], float(a), None, A.is_equal)
+    ka16 = copy([], T.act16[:], T.acti[:])
+    kcb = copy([tcap], T.capb[:], T.capf[:])
+    kp = tt([tnx, km], T.prod[:], T.nxi[:], T.m3[:], A.mult)
+    thirds = [T.prod[:, a * M:a * M + M] for a in range(NA)]
+    group([kp, kpa], B[1][:, 0:M], [(T.pa[:], x) for x in thirds])
+    pAB = group([kpb], B[1][:, M:2 * M], [(T.pb[:], x) for x in thirds])
+    pT = group([kid], B[0][:, 0:M], [(idb, x) for x in thirds])
+    kn0 = copy([], T.nxu[:], T.nxi[:])
+    kdig = digits([pAB], B[1][:, 0:2 * M], T.yt[:], T.ys[:], T.yd[:])
+    pun = [group([kdig], B[2 + n // 4][:, n % 4 * M:n % 4 * M + M], [(T.idz[:, n % 8:n % 8 + 128], T.yd[:, n // 8 * M:n // 8 * M + M])])
+           for n in range(16)]
+    ku0 = copy([pT], U[0][:], B[0][:, 0:M])
+    ki1 = tsc([kid], T.i1[:], idb, float(S), None, A.mult)
+    kpm = tsc([kpi], T.pm[:], T.pi[:], 15, None, A.bitwise_and)
+    kpf = copy([kpm], T.pf[:], T.pm[:])
+    kst = tsc([kpf, ksti], T.st16[:], T.sti[:], T.pf[:], None, A.add)
+    pL = group([ki1, kst, ka16], B[6][:, 0:M], [(T.i1[:], T.act16[:]), (idb, T.st16[:])])
+    kt0 = []
+    for n in range(16):
+        kt0.append((copy if n // 4 % 2 else act)([pun[n // 4 * 4 + 3]], TD[0][:, n::16], B[2 + n // 4][:, n % 4 * M:n % 4 * M + M]))
+    kl = copy([pL], T.lu[:], B[6][:, 0:M])
+    psc = group([kzq, kcb], B[7][:, 0:1], [(T.zq[:, 15 - i:143 - i], T.capb[:]) for i in range(16)])
+    pe = fold([trw[0], trw[1], kl], B[6][:, 0:2 * M], T.zq, T.rwb, 0, 2 * S)
+
+    def caps(n):
+        return act([trw[n // 2], tcap], T.db[:, n * H:n * H + H], T.rwb[:, n * H:n * H + H], F.Identity, T.capf[:], -1.0)
+
+    def cols(x):
+        a, b = BLK[x]
+        return a, b, 2 * a, a + b, 2 * b
+
+    def presum(rnd, x, deps):
+        a, b, c0, c1, c2 = cols(x)
+        bank = B[7 if x == 0 else 0][:, 0:c2 - c0]
+        mm(deps, bank, idb, T.eo[:, c0:c2], True, False)
+        for p in before:
+            mm([("ae%d" % p, arrival)], bank, idb, T["ev%d" % p][:, c0:c2], False, False)
+
+    def total(rnd, x, ko):
+        a, b, c0, c1, c2 = cols(x)
+        bank = B[7 if x == 0 else 0][:, 0:c2 - c0]
+        mm([ko], bank, idb, T["o%d" % rnd][:, c0:c2], False, False)
+        for n, p in enumerate(before):
+            k = mm([("a%d_%d_%d" % (rnd, x, p), arrival)], bank, idb, T["v%d_%d" % (rnd, p)][:, c0:c2], False, n == NR - 2)
+        return k
+
+    def choose(x, pD):
+        a, b, c0, c1, c2 = cols(x)
+        bank, n = B[7 if x == 0 else 0], b - a
+        tsc([pD], T.wm[:, c0:c1], bank[:, n:2 * n], -40000.0, 0.0, A.mult, A.min)
+        kw = tsc([], T.wm[:, c1:c2], bank[:, 0:n], 0.0, None, A.max)
+        return tt([kw], T.bb[:, c0:c2], bank[:, 0:2 * n], T.wm[:, c0:c2], A.is_gt)
+
+    def places(x, kb, deps):
+        a, b, c0, c1, c2 = cols(x)
+        bank = B[1 if x == 0 else 5][:, 0:b - a]
+        mm(deps, bank, idb, T.st16[:, a:b], True, False)
+        mm([kb], bank, T.i1[:], T.bb[:, c0:c1], False, False)
+        p = mm([], bank, T.i1[:], T.bb[:, c1:c2], False, True)
+        return copy([p], T.lu[:, a:b], bank)
+
+    def tstep(k, h, deps, free):
+        a, b = h * H, h * H + H
+        t = act(deps, TD[k][:, a:b], TD[k - 1][:].indirect(U[k - 1][:, a // 16:b // 16]))
+        return t, fold([t, kzx] + free, B[h][:, 0:M // 2], T.zx, TD[k], a, b)
+
+    def tlist(k, h, p):
+        return copy([p], U[k][:, h * M // 2:h * M // 2 + M // 2], B[h][:, 0:M // 2])
+
+    def rstep(k, a, b, deps):
+        return tt(deps, R[k][:, a:b], R[k - 1][:].indirect(U[k - 1][:, a // 16:b // 16]), K[k - 1][:, a:b], A.add)
+
+    pD, ko, kx, kre, xdt = None, None, None, None, []
     for rnd in range(ROUNDS):
         first, last = rnd == 0, rnd == ROUNDS - 1
-        pL = group(tb_ + [ki1, ki2, kst], T.b5[:, 0:96],
-                   [(T.i1[:], T.bb[:, 0:96]), (T.i2[:], T.bb[:, 96:192]), (T.idb[:], T.st16[:])])
-        kpr = tt(tb_ + kdn, T.pr[:], T.bb[:], T.dn[:], A.mult)
-        kl = copy([pL], T.lu[:], T.b5[:, 0:96])
-        pT = group([kpr], T.b0[:, 0:96], [(T.idb[:], T.nx16[:, 0:96]), (T.idb[:], T.pr[:, 0:96]), (T.idb[:], T.pr[:, 96:192])])
-        kt = act([kl] + (xdt if first else []), T.ta[:], T.xd[:].indirect(T.lu[:]))
+        ul, tk, pf_ = {}, {}, {}
         if first:
-            kd = [caps("V", 0), None, caps("V", 2)]
-        wait("V", kl, *trw)
-        kr = [copy([], T.ra[:, 0:RC[0]], T.rwb[:].indirect(T.lu[:, 0:RC[0] // 16]))]
-        ktu = copy([pT], T.tu0[:], T.b0[:, 0:96])
-        kr.append(copy([], T.ra[:, RC[0]:S], T.rwb[:].indirect(T.lu[:, RC[0] // 16:M])))
-        krk = [copy(kr, T.rk[:], T.ra[:])]
-        if first:
-            knz = tsc([kzq], T.nzq[:], T.zq[:], -1.0, None, A.mult)
-            pe = [fold([trw[a], kzq] + xdt, T["b%d" % (1 + a)][:, 0:MV], T.zq, T.rwb, a * S, a * S + NV) for a in range(NA)]
-
-        def preload():
-            for a in range(NA):
-                mm([kid], T["b%d" % (1 + a)][:, 0:NS], T.idb[:], T.rwb[:, a * S + NV:a * S + S], True, False)
-
-        if not first:
-            preload()
-        cur = 0
-        ktx = [kt]
-        for st in range(3):
-            tc, tn, rc, rn, tu, tun = T_[cur], T_[1 - cur], R_[cur], R_[1 - cur], TU[cur], TU[1 - cur]
-            tv, tf, rcut = TV[st], TF[st], RC[st]
-            hv = [copy([ktu] + ktx, tn[:, 0:tv], tc[:].indirect(tu[:, 0:tv // 16]))] if tv else []
-            h1 = act([ktu] + ktx, tn[:, tv:tf], tc[:].indirect(tu[:, tv // 16:tf // 16]))
-            h2 = act([], tn[:, tf:S], tc[:].indirect(tu[:, tf // 16:M]))
-            ktx = hv + [h2]
-            fold(hv + [h1, kzx], T.b0[:, 0:tf // 16], T.zx, tn, 0, tf)
-            px = fold([h2], T.b0[:, tf // 16:M], T.zx, tn, tf, S)
-            k1 = tt(kr + krk + [ktu], rn[:, 0:rcut], rc[:].indirect(tu[:, 0:rcut // 16]), T.rk[:, 0:rcut], A.add)
-            k2 = tt([], rn[:, rcut:S], rc[:].indirect(tu[:, rcut // 16:M]), T.rk[:, rcut:S], A.add)
-            kr = [k2]
-            krk = [act([k1], T.rk[:, 0:rcut], rn[:, 0:rcut])]
-            if st < 2:
-                krk.append(copy([k2], T.rk[:, rcut:S], rn[:, rcut:S]))
-            if first and st == 0:
-                k = copy([pe[0]], T.x0[:], T.b1[:, 0:MV])
-                tt([k, pe[1]], T.eo[:, 0:MV], T.b2[:, 0:MV], T.x0[:], A.subtract)
-                ke = tt([pe[2]], T.eo[:, MV:2 * MV], T.b3[:, 0:MV], T.x0[:], A.subtract)
-                sent += share([ke], T.eo[:], T["ev%d" % rank][:], "ae%d" % rank)
-            ktu = copy([px], tun[:], T.b0[:, 0:96])
-            cur = 1 - cur
-        rc, rn, tu = R_[cur], R_[1 - cur], TU[cur]
-        mm(kr, T.b6[:, 0:S - RS], T.idb[:], rc[:, RS:S], True, False)
-        hz = act([ktu] + kr, T.zr[:], rc[:].indirect(tu[:, RS // 16:M]))
-        pz = mm([hz], T.b6[:, 0:S - RS], T.idb[:], T.zr[:], False, True)
-        ks = act([pz], rn[:, RS:S], T.b6[:, 0:S - RS])
-        kv = tt([ktu] + kr + krk, rn[:, 0:RS], rc[:].indirect(tu[:, 0:RS // 16]), T.rk[:, 0:RS], A.add)
-        if first:
-            wait("P", ke)
-            preload()
-            kd[1] = caps("S", 1)
-        hz = [act([kv, ks, kn0], T.zs[:, a * NS:a * NS + NS], rn[:].indirect(T.nxu[:, a * M + MV:a * M + M])) for a in range(NA)]
-        pz = [mm([hz[a]], T["b%d" % (1 + a)][:, 0:NS], T.idb[:], T.zs[:, a * NS:a * NS + NS], False, True) for a in range(NA)]
-        wait("S", tcap)
-        kre = [act([pz[a]], T.ts[:, a * NS:a * NS + NS], T["b%d" % (1 + a)][:, 0:NS], F.Relu, T.capf[:], -1.0) for a in range(NA)]
-        hv = [tt([kv, ks, kd[a]], T["tv%d" % a][:], rn[:].indirect(T.nxu[:, a * M:a * M + MV]), T.db[:, a * NV:a * NV + NV], A.min)
-              for a in range(NA)]
-        pv0 = fold([hv[0], kzq], T.b4[:, 0:MV], T.zq, T.tv0, 0, NV)
-        if first:
-            pv1 = fold([hv[1]], T.b5[:, 0:MV], T.zq, T.tv1, 0, NV)
-        ps = fold([kre[2], knz], T.b7[:, 0:3 * MS], T.nzq, T.ts, 0, 3 * NS)
-        if not first:
-            pv1 = fold([hv[1]], T.b5[:, 0:MV], T.zq, T.tv1, 0, NV)
-        pv2 = fold([hv[2]], T.b6[:, 0:MV], T.zq, T.tv2, 0, NV)
-        kx0 = act([pv0], T.x0[:], T.b4[:, 0:MV])
-        kx1 = act([ps], T.xs0[:], T.b7[:, 0:MS])
+            ul[0, 0] = ul[0, 1] = ku0
+            tk[1, 0], pf_[1, 0] = tstep(1, 0, [ku0] + kt0, [ku0])
+            tk[1, 1], pf_[1, 1] = tstep(1, 1, [], [kdig])
+            ksc = act([psc], T.nsc[:], B[7][:, 0:1])
+            kd = [caps(0)]
+            ra = copy([kl] + trw, R[0][:, 0:SA], T.rwb[:].indirect(T.lu[:, 0:MA]))
+            kc = {(0, 0): dup("G", [ra], 0, 0, XG0)}
+            rb = copy([], R[0][:, SA:S], T.rwb[:].indirect(T.lu[:, MA:M]))
+            ul[1, 0] = tlist(1, 0, pf_[1, 0])
+            tk[2, 0], pf_[2, 0] = tstep(2, 0, [ul[1, 0], tk[1, 1]], [ul[1, 0]])
+            kv = dup("V", [ra], 0, XG0, SA)
+            free2 = kt0
+        else:
+            kla = places(0, choose(0, pD[0]), [ko[0]])
+            ta = act([kla] + xdt, TD[0][:, 0:SA], T.xd[:].indirect(T.lu[:, 0:MA]))
+            ra = copy([kla], R[0][:, 0:SA], T.rwb[:].indirect(T.lu[:, 0:MA]))
+            kc = {(0, 0): dup("G", [ra], 0, 0, XG0)}
+            pD1 = total(rnd - 1, 1, ko[1])
+            kv = dup("V", [ra], 0, XG0, SA)
+            kb = choose(1, pD1)
+            klb = places(1, kb, [kx[1]])
+            pa_ = fold([ta, ko[1]] + xdt, B[6][:, 0:MA], T.zx, TD[0], 0, SA)
+            tb = act([klb], TD[0][:, SA:S], T.xd[:].indirect(T.lu[:, MA:M]))
+            pb_ = fold([tb], B[7][:, 0:M - MA], T.zx, TD[0], SA, S)
+            rb = copy([klb], R[0][:, SA:S], T.rwb[:].indirect(T.lu[:, MA:M]))
+            ul[0, 0] = copy([pa_], U[0][:, 0:MA], B[6][:, 0:MA])
+            tk[0, 1] = tb
+            free2 = kre + xdt
+        kc[0, 0] += kv
+        kc[0, 1] = kv + dup("G", [rb], 0, SA, S)
+        kr = rb
+        for a in range(3):
+            mm(free2 + [trw[2]], B[2 + a][:], idb, T.rwb[:, 2 * S + 512 * a:2 * S + 512 * a + 512], True, False)
+        for k in (1, 2, 3):
+            for h in range(2):
+                a = h * H
+                lo = a if k < 3 or h else RS
+                if not first:
+                    tk[k, h], pf_[k, h] = tstep(k, h, [ul[k - 1, h], tk[k - 1, 1]], [ul[k - 1, h], kb])
+                r = rstep(k, a, a + H, [kr, ul[k - 1, h]] + kc[k - 1, h])
+                if h:
+                    kr = r
+                xg = 0 if first and k > EAT else XG
+                xs = 0 if first else XS
+                kc[k, h] = dup("G", [r], k, lo, min(lo + xg, a + H))
+                kc[k, h] += dup("S", [r], k, lo + xg, min(lo + xg + xs, a + H))
+                if first:
+                    if (k, h) == (EAT, 1):
+                        share([ke], T.eo[:], T["ev%d" % rank][:], "ae%d" % rank)
+                    kt, ht = {(1, 0): (1, 1), (1, 1): (2, 0), (2, 1): (2, 1), (3, 0): (3, 0)}.get((k, h), (0, 0))
+                    if kt:
+                        ul[kt, ht] = tlist(kt, ht, pf_[kt, ht])
+                    if 0 < kt < 3:
+                        kd.append(caps(len(kd)))
+                        tk[kt + 1, ht], pf_[kt + 1, ht] = tstep(kt + 1, ht, [ul[kt, ht], tk[kt, 1]], [ul[kt, ht]])
+                    if (k, h) == (1, 0):
+                        for x in range(2):
+                            a0, b0, c0, c1, c2 = cols(x)
+                            ke = tsc([pe], T.eo[:, c1:c2], B[6][:, a0:b0], -1.0, None, A.mult)
+                        for x in range(2):
+                            a0, b0, c0, c1, c2 = cols(x)
+                            ke = tt([ke], T.eo[:, c0:c1], B[6][:, M + a0:M + b0], T.eo[:, c1:c2], A.add)
+                elif h == 0:
+                    ul[k - 1, 1] = copy([pb_], U[0][:, MA:M], B[7][:, 0:M - MA]) if k == 1 else tlist(k - 1, 1, pf_[k - 1, 1])
+                else:
+                    ul[k, 0] = tlist(k, 0, pf_[k, 0])
+                kc[k, h] += dup("V", [r], k, lo + xg + xs, a + H)
+        mm([kr] + kt0 + ([] if first else [klb]), B[5][:, 0:RS], idb, R[3][:, 0:RS], True, False)
+        hz = act([kr, ul[3, 0]], T.zr[:], R[3][:].indirect(U[3][:, 0:RS // 16]))
+        pz = mm([hz], B[5][:, 0:RS], idb, T.zr[:], False, True)
+        ks = act([pz], R[4][:, 0:RS], B[5][:, 0:RS])
+        rstep(4, RS, H, [kr, ul[3, 0]] + kc[3, 0])
+        ul[3, 1] = tlist(3, 1, pf_[3, 1])
+        kv = rstep(4, H, S, [ul[3, 1]] + kc[3, 1])
         o = T["o%d" % rnd]
-        tt([kx1], o[:, MV:M], T.b7[:, MS:2 * MS], T.xs0[:], A.subtract)
-        tt([], o[:, M + MV:2 * M], T.b7[:, 2 * MS:3 * MS], T.xs0[:], A.subtract)
-        tt([pv1, kx0], o[:, 0:MV], T.b5[:, 0:MV], T.x0[:], A.subtract)
-        ko = tt([pv2], o[:, M:M + MV], T.b6[:, 0:MV], T.x0[:], A.subtract)
-        sent += share([ko], o[:], T["v%d_%d" % (rnd, rank)][:], "a%d_%d" % (rnd, rank))
+
+        def vsum(a, x, deps):
+            a0, b0 = BLK[x]
+            return tt(deps, T["tv%d" % a][:, 16 * a0:16 * b0], R[4][:].indirect(T.nxu[:, a * M + a0:a * M + b0]),
+                      T.db[:, a * S + 16 * a0:a * S + 16 * b0], A.min)
+
+        def sgather(n):
+            z = act([kv, ks, kn0], T.zs[:, 512 * n:512 * n + 512], R[4][:].indirect(T.nxu[:, 2 * M + 32 * n:2 * M + 32 * n + 32]))
+            return mm([z], B[2 + n][:], idb, T.zs[:, 512 * n:512 * n + 512], False, True)
+
+        def srelu(n, p):
+            return act([p], T.ts[:, 512 * n:512 * n + 512], B[2 + n][:], F.Relu, T.capf[:], -1.0)
+
+        def base(x, p, bank):
+            a0, b0, c0, c1, c2 = cols(x)
+            act([p], T.x0[:, c0:c1], bank[:, 0:b0 - a0])
+            return act([ksc], T.x0[:, c1:c2], bank[:, 0:b0 - a0], F.Identity, T.nsc[:], -1.0)
+
+        def differ(x, kx0, pp_, p1, bank):
+            a0, b0, c0, c1, c2 = cols(x)
+            n = b0 - a0
+            tt([kx0, pp_, p1], o[:, c1:c2], T.x0[:, c1:c2], bank[:, n:2 * n], A.subtract)
+            k = tt([], o[:, c0:c1], bank[:, 0:n], T.x0[:, c0:c1], A.subtract)
+            share([k], o[:, c0:c2], T["v%d_%d" % (rnd, rank)][:, c0:c2], "a%d_%d_%d" % (rnd, x, rank))
+            return k
+
+        h0a = vsum(0, 0, [kv, ks] + kd)
+        h1a = vsum(1, 0, [])
+        h0b = vsum(0, 1, [])
+        z = [sgather(0), sgather(1)]
+        kre = [srelu(0, z[0]), srelu(1, z[1])]
+        p0a = fold([h0a, kzq, ul[3, 0]], B[0][:, 0:MA], T.zq, T.tv0, 0, SA)
+        ppa = fold([kre[1], ul[3, 1]], B[1][:, MA:2 * MA], T.zq, T.ts, 0, SA)
+        p1a = fold([h1a], B[1][:, 0:MA], T.zq, T.tv1, 0, SA)
+        kx = [base(0, p0a, B[0])]
+        z2 = sgather(2)
+        kre.append(srelu(2, z2))
+        ko = [differ(0, kx[0], ppa, p1a, B[1])]
+        h1b = vsum(1, 1, [])
+        p0b = fold([h0b, ks], B[5][:, 0:M - MA], T.zq, T.tv0, SA, S)
+        ppb = fold([kre[2], ke, ul[0, 0]], B[6][:, M - MA:2 * (M - MA)], T.zq, T.ts, SA, S)
+        p1b = fold([h1b], B[6][:, 0:M - MA], T.zq, T.tv1, SA, S)
+        kx.append(base(1, p0b, B[5]))
+        ko.append(differ(1, kx[1], ppb, p1b, B[6]))
+        if not first:
+            presum(rnd, 0, [ke, ksc, ul[0, 1]])
+            presum(rnd, 1, [kx[0]])
+        if first:
+            t16 = copy([], T.nx16[:], T.nxi[:])
+            pA = group([t16] + kre, B[2][:, 0:288], [(T.pa[:], T.nx16[:])])
+            pB = group([], B[3][:, 0:288], [(T.pb[:], T.nx16[:])])
+            dig = [digits([p], B[2 + h][:, 0:288], T.xt[:, 288 * h:288 * h + 288], T.xs[:, 288 * h:288 * h + 288],
+                          T.xb[:, 288 * h:288 * h + 288]) for h, p in enumerate((pA, pB))]
+            free = {4: [], 6: [ko[1]], 2: [dig[0]], 3: [dig[1]]}
+            for n in range(16):
+                h, j = n // 8, n % 8
+                b = (4, 6, 2)[n % 3] if n < 6 else (4, 6, 2, 3)[(n - 6) % 4]
+                if n == 4:
+                    presum(rnd, 0, [ke, ksc, ul[0, 1]])
+                    presum(rnd, 1, [kx[0]])
+                if n == 12:
+                    pD = [total(rnd, 0, ko[0])]
+                tok = group([dig[h]] + free[b], B[b][:, 0:288], [(T.idz[:, j:j + 128], T.xb[:, 288 * h:288 * h + 288])])
+                mine = n >= 16 - 2 * XDV and n % 2 == 0
+                free[b] = [(copy if mine else act)([tok], T.xd[:, n::16], B[b][:, 0:288])]
+                xdt += free[b]
+        else:
+            pD = [total(rnd, 0, ko[0])]
         if last:
-            wait("V", tcap)
-            ky = tsc([kv, ks], T.yb[:], rn[:], T.capf[:], None, A.min)
+            ky = tsc([kv, ks, tcap], T.yb[:], R[4][:], T.capf[:], None, A.min)
             wait("Y", ky)
             sy = load("Y", "st0", T.yr[:], T.yb[:])
-        if first:
-            mm([ke, ko], T.b7[:, 0:2 * MV], T.idb[:], T.eo[:], True, False)
-            for n, p in enumerate(before):
-                k = mm([("ae%d" % p, 8)], T.b7[:, 0:2 * MV], T.idb[:], T["ev%d" % p][:], False, n == NR - 2)
-            copy([k], T.eg[:, 0:MV], T.b7[:, 0:MV])
-            keg = copy([], T.eg[:, M:M + MV], T.b7[:, MV:2 * MV])
-        mm([keg, ko], T.b4[:, 0:192], T.idb[:], T.eg[:], True, False)
-        mm([], T.b4[:, 0:192], T.idb[:], o[:], False, False)
-        for n, p in enumerate(before):
-            pD = mm([("a%d_%d" % (rnd, p), 8)], T.b4[:, 0:192], T.idb[:], T["v%d_%d" % (rnd, p)][:], False, n == NR - 2)
-        tsc([pD], T.wm[:, 0:96], T.b4[:, 96:192], -1.0, 0.0, A.add, A.max)
-        kw = tsc([], T.wm[:, 96:192], T.b4[:, 0:96], 0.0, None, A.max)
-        kb = tt([kw], T.bb[:], T.b4[:, 0:192], T.wm[:], A.is_gt)
-        tb_ = [kb]
-    k = tsc([kb], T.yt[:], T.bb[:, 96:192], 2.0, None, A.mult)
-    k = tt([k], T.yf[:], T.yt[:], T.bb[:, 0:96], A.add)
+    for x in range(2):
+        a, b, c0, c1, c2 = cols(x)
+        kb = choose(x, pD[0] if x == 0 else total(ROUNDS - 1, 1, ko[1]))
+        k = tt([kb], T.yf[:, a:b], T.bb[:, c0:c1], T.bb[:, c1:c2], A.add)
     wait("Y", k)
     sa = load("Y", "st1", T.ya[:], T.yf[:])
     wait("Y", sy, sa)
-    wait("G", ("loc", sent), ("cV", count["V"]), ("cS", count["S"]), ("cP", count["P"]), ("cG", count["G"]))
+    wait("G", ("loc", sent[0]), ("cV", count["V"]), ("cS", count["S"]), ("cP", count["P"]), ("cG", count["G"]))

@@ -5,31 +5,37 @@ NR, ROUNDS = 8, 3
 S, NA = 1536, 3
 M = S // 16
 H = S // 2
-MA = 64
-SA = 16 * MA
+MA = 56
+SA, MB = 16 * MA, M - MA
+SB = S - SA
 BLK = ((0, MA), (MA, M))
-XG, XS = 384, 192
-XG0 = 640
-RS = 512
-EAT = 2
-XDV = 5
+PIECES = ((0, SA // 2, 2), (SA // 2, SA, 3), (SA, min(SA + 512, S), 4), (SA + 512, S, 7))[:3 if SB <= 512 else 4]
+OPT = dict(z2=0, add2=0, sub=0)
+XG, XS = 448, 160
+XG3 = 384
+XG0, XG1 = 512, 448
+R0S = 224
+RS, RT = 256, 192
+GK = 3
+XS0, XS1 = 512, (384, 512, 320)
+CV = 2
 
 _B, _H, _F, _I, _U = "bfloat16", "float16", "float32", "int32", "uint16"
 SCRATCH = {
     "nxi": ("sbuf", [128, 288], _I), "acti": ("sbuf", [128, 96], _I), "capf": ("sbuf", [128, 1], _F),
     "rwb": ("sbuf", [128, 4608], _B), "db": ("sbuf", [128, 2 * S], _B), "xd": ("sbuf", [128, 4608], _B),
-    "nx16": ("sbuf", [128, 288], _H), "nxu": ("sbuf", [128, 288], _U), "m3": ("sbuf", [128, 288], _H),
-    "prod": ("sbuf", [128, 288], _H), "act16": ("sbuf", [128, 96], _B),
-    "xt": ("sbuf", [128, 576], _I), "xs": ("sbuf", [128, 576], _I), "xb": ("sbuf", [128, 576], _B),
-    "yt": ("sbuf", [128, 192], _I), "ys": ("sbuf", [128, 192], _I), "yd": ("sbuf", [128, 192], _B),
-    "lu": ("sbuf", [128, 96], _U), "sti": ("sbuf", [128, 96], _I), "pi": ("sbuf", [128, 1], _I), "pm": ("sbuf", [128, 1], _I),
-    "pf": ("sbuf", [128, 1], _F), "st16": ("sbuf", [128, 96], _H), "capb": ("sbuf", [128, 1], _B), "nsc": ("sbuf", [128, 1], _F),
+    "nx16": ("sbuf", [128, 288], _H), "nxh": ("sbuf", [128, 288], _B), "nxu": ("sbuf", [128, 288], _U),
+    "m3": ("sbuf", [128, 288], _H), "prod": ("sbuf", [128, 288], _H), "act16": ("sbuf", [128, 96], _B),
+    "nxl": ("sbuf", [128, 288], _B), "th": ("sbuf", [128, 96], _B), "yd": ("sbuf", [128, 192], _B),
+    "lu": ("sbuf", [128, 192], _U), "sti": ("sbuf", [128, 192], _I), "pi": ("sbuf", [128, 1], _I),
+    "pm": ("sbuf", [128, 12], _I), "pc": ("sbuf", [128, 20], _F),
+    "nid": ("sbuf", [128, 128], _B), "i2": ("sbuf", [128, 128], _B), "row": ("sbuf", [128, 64], _H),
+    "st16": ("sbuf", [128, 192], _H), "capb": ("sbuf", [128, 1], _B), "nsc": ("sbuf", [128, 1], _F),
     "bb": ("sbuf", [128, 192], _H), "wm": ("sbuf", [128, 192], _F),
-    "zr": ("sbuf", [128, RS], _B), "tv0": ("sbuf", [128, S], _B), "tv1": ("sbuf", [128, S], _B),
-    "zs": ("sbuf", [128, S], _B), "ts": ("sbuf", [128, S], _B),
+    "zr": ("sbuf", [128, S], _B), "qs": ("sbuf", [128, 2 * S], _B), "tv0": ("sbuf", [128, S], _B), "zs": ("sbuf", [128, S], _B),
     "x0": ("sbuf", [128, 192], _F), "eo": ("sbuf", [128, 192], _H),
     "yb": ("sbuf", [128, S], _B), "yf": ("sbuf", [128, 96], _F),
-    "pa": ("sbuf", [128, 128], _B), "pb": ("sbuf", [128, 128], _B), "idz": ("sbuf", [128, 136], _B), "i1": ("sbuf", [128, 128], _B),
+    "cut": ("sbuf", [128, 768], _B), "idz": ("sbuf", [128, 144], _B), "i1": ("sbuf", [128, 128], _B),
     "zx": ("sbuf", [128, 144], _B), "zq": ("sbuf", [128, 144], _B),
 }
 for _k in range(5):
@@ -45,7 +51,7 @@ for _r in range(ROUNDS):
     SCRATCH["o%d" % _r] = ("sbuf", [128, 192], _H)
     for _k in range(NR):
         SCRATCH["v%d_%d" % (_r, _k)] = ("sbuf", [128, 192], _H)
-SEMAPHORES = ["cV", "cS", "cP", "cG", "lnx", "lact", "lcap", "lrw0", "lrw1", "lrw2", "st0", "st1", "loc"]
+SEMAPHORES = ["cV", "cS", "cP", "cG", "lnx", "lact", "lcap", "lrw0", "lrw1", "lrw2", "st0", "st1", "loc", "lxd", "lxh", "lxl"]
 SEMAPHORES += ["ae%d" % k for k in range(NR)]
 SEMAPHORES += ["a%d_%d_%d" % (r, x, k) for r in range(ROUNDS) for x in range(2) for k in range(NR)]
 
@@ -60,7 +66,7 @@ def rank_program(g, core, T, topo):
     seen = {}
     B = [T["b%d" % n] for n in range(8)]
     R, K, TD, U = ([T["%s%d" % (c, n)] for n in range(k)] for c, k in (("r", 5), ("k", 4), ("t", 4), ("u", 4)))
-    idb = T.idz[:, 0:128]
+    idb = T.idz[:, 8:136]
 
     def wait(q, *toks):
         for name, val in toks:
@@ -124,11 +130,6 @@ def rank_program(g, core, T, topo):
         wait("G", *deps)
         return [mark("G", g.affine_select(K[k][:, a:b], R[k][:, a:b], [[0, b - a]], A.is_ge, 0.0, 0, 0))]
 
-    def digits(deps, src, ti, si, out):
-        a = copy(deps, ti, src)
-        b = tsc([a], si, ti, 8, 255, A.logical_shift_right, A.bitwise_and)
-        return copy([b], out, si)
-
     others = [T.cores[(rank + n) % NR] for n in range(1, NR)]
     before = [(rank - n) % NR for n in range(1, NR)]
     sent = [0]
@@ -152,58 +153,81 @@ def rank_program(g, core, T, topo):
     tcap = load("S", "lcap", T.capf[:], T.cap[:])
     trw = [load("Y", "lrw%d" % a, T.rwb[:, a * S:(a + 1) * S], T.rw[:, a * S:(a + 1) * S]) for a in range(NA)]
 
-    zero = {}
-    for n in ("pa", "pb", "idz", "zx"):
-        zero[n] = mark("V", V.memset(T[n][:], 0.0))
-    zero["zq"] = mark("V", V.memset(T.zq[:], 1.0))
-    pp = [[-16, 8], [1000, 2], [-1, 8]]
-    k = pick(zero["pa"], "pa", pp, A.not_equal, 256.0, 0, 1)
-    kpa = pick(k, "pa", pp, A.not_equal, 1.0, -1000, 1)
-    k = pick(zero["pb"], "pb", pp, A.not_equal, 256.0, -8, 1)
-    kpb = pick(k, "pb", pp, A.not_equal, 1.0, -1008, 1)
-    kid = pick(zero["idz"], "idz", [[-1, 136]], A.not_equal, 1.0, 0, 1)
-    kpi = mark("G", g.iota(T.pi[:], [[1, 1]], 0, 1))
-    ksti = mark("G", g.iota(T.sti[:], [[16, 96]], 0, 0))
-    k = pick(zero["zx"], "zx", [[-16, 9], [1000, 16]], A.not_equal, 1.0, -15000, 1)
-    kzx = pick(k, "zx", [[-16, 9], [1000, 16]], A.not_equal, 256.0, -15008, 1)
-    k = pick(zero["zq"], "zq", [[0, 9], [1, 16]], A.is_ge, 0.0, -15, 0)
-    k = pick(k, "zq", [[-16, 9], [0, 16]], A.is_ge, 0.0, 0, 1)
-    kzq = pick(k, "zq", [[16, 9], [0, 16]], A.is_ge, 0.0, 15, -1)
-
-    for a in range(NA):
-        km = tsc([tact], T.m3[:, a * M:a * M + M], T.acti[:], float(a), None, A.is_equal)
-    ka16 = copy([], T.act16[:], T.acti[:])
-    kcb = copy([tcap], T.capb[:], T.capf[:])
-    kp = tt([tnx, km], T.prod[:], T.nxi[:], T.m3[:], A.mult)
-    thirds = [T.prod[:, a * M:a * M + M] for a in range(NA)]
-    group([kp, kpa], B[1][:, 0:M], [(T.pa[:], x) for x in thirds])
-    pAB = group([kpb], B[1][:, M:2 * M], [(T.pb[:], x) for x in thirds])
-    pT = group([kid], B[0][:, 0:M], [(idb, x) for x in thirds])
-    kn0 = copy([], T.nxu[:], T.nxi[:])
-    kdig = digits([pAB], B[1][:, 0:2 * M], T.yt[:], T.ys[:], T.yd[:])
-    pun = [group([kdig], B[2 + n // 4][:, n % 4 * M:n % 4 * M + M], [(T.idz[:, n % 8:n % 8 + 128], T.yd[:, n // 8 * M:n // 8 * M + M])])
-           for n in range(16)]
-    ku0 = copy([pT], U[0][:], B[0][:, 0:M])
-    ki1 = tsc([kid], T.i1[:], idb, float(S), None, A.mult)
-    kpm = tsc([kpi], T.pm[:], T.pi[:], 15, None, A.bitwise_and)
-    kpf = copy([kpm], T.pf[:], T.pm[:])
-    kst = tsc([kpf, ksti], T.st16[:], T.sti[:], T.pf[:], None, A.add)
-    pL = group([ki1, kst, ka16], B[6][:, 0:M], [(T.i1[:], T.act16[:]), (idb, T.st16[:])])
-    kt0 = []
-    for n in range(16):
-        kt0.append((copy if n // 4 % 2 else act)([pun[n // 4 * 4 + 3]], TD[0][:, n::16], B[2 + n // 4][:, n % 4 * M:n % 4 * M + M]))
-    kl = copy([pL], T.lu[:], B[6][:, 0:M])
-    psc = group([kzq, kcb], B[7][:, 0:1], [(T.zq[:, 15 - i:143 - i], T.capb[:]) for i in range(16)])
-    pe = fold([trw[0], trw[1], kl], B[6][:, 0:2 * M], T.zq, T.rwb, 0, 2 * S)
-
-    def caps(n):
-        return act([trw[n // 2], tcap], T.db[:, n * H:n * H + H], T.rwb[:, n * H:n * H + H], F.Identity, T.capf[:], -1.0)
-
     def cols(x):
         a, b = BLK[x]
         return a, b, 2 * a, a + b, 2 * b
 
-    def presum(rnd, x, deps):
+    kz = mark("V", V.memset(T.idz[:], 0.0))
+    kq = mark("V", V.memset(T.zq[:], 1.0))
+    kpi = mark("G", g.iota(T.pi[:], [[1, 1]], 0, 1))
+    kid = pick(kz, "idz", [[-1, 144]], A.not_equal, 1.0, 8, 1)
+    mark("G", g.iota(T.sti[:, 0:M], [[16, M]], 0, 0))
+    ksti = mark("G", g.iota(T.sti[:, M:2 * M], [[1, M]], 0, 0))
+    k = pick(kq, "zq", [[0, 9], [1, 16]], A.is_ge, 0.0, -15, 0)
+    k = pick(k, "zq", [[-16, 9], [0, 16]], A.is_ge, 0.0, 0, 1)
+    kzq = pick(k, "zq", [[16, 9], [0, 16]], A.is_ge, 0.0, 15, -1)
+    for n, bits in enumerate((15, 8, 7)):
+        k = tsc([kpi], T.pm[:, 4 * n:4 * n + 1], T.pi[:], bits, None, A.bitwise_and)
+    p16, low, high, head = (T.pc[:, 4 * n:4 * n + 1] for n in range(4))
+    copy([k], p16, T.pm[:, 0:1])
+    tsc([], low, T.pm[:, 4:5], 0.0, None, A.is_equal)
+    tsc([], high, T.pm[:, 4:5], 8.0, None, A.is_equal)
+    kpc = tsc([], head, T.pm[:, 8:9], 0.0, None, A.is_equal)
+    cut = [T.cut[:, 128 * n:128 * n + 128] for n in range(6)]
+    for n, (c, half, sign) in enumerate(((8, low, 1.0), (8, low, -1.0), (0, low, 1.0), (16, high, 1.0), (16, high, -1.0), (8, high, 1.0))):
+        kcut = tsc([kid, kpc], cut[n], T.idz[:, c:c + 128], half, sign, A.mult, A.mult)
+    tsc([], T.i1[:], idb, float(S), None, A.mult)
+    tsc([], T.i2[:], idb, float(M), None, A.mult)
+    tsc([], T.nid[:], idb, -1.0, None, A.mult)
+    k = tsc([], T.pc[:, 16:17], p16, 288.0, None, A.mult)
+    for x in range(2):
+        a, b, c0, c1, c2 = cols(x)
+        tsc([ksti], T.st16[:, c0:c1], T.sti[:, a:b], p16, None, A.add)
+        copy([], T.st16[:, c1:c2], T.sti[:, M + a:M + b])
+    kst = tsc([k], T.row[:], T.sti[:, 0:64], 0.0, T.pc[:, 16:17], A.mult, A.add)
+
+    def unfold(deps, out, n, src, width):
+        j = n % 8
+        return group(deps, out, [(T.idz[:, 8 + j:136 + j], src[:, n // 8 * width:n // 8 * width + width])])
+
+    for a in range(NA):
+        km = tsc([tact], T.m3[:, a * M:a * M + M], T.acti[:], float(a), None, A.is_equal)
+    ka16 = copy([], T.act16[:], T.acti[:])
+    for x in range(2):
+        a, b, c0, c1, c2 = cols(x)
+        pL = group([kst, ka16], B[6][:, a:b], [(T.i1[:], T.act16[:, a:b]), (idb, T.st16[:, c0:c1])])
+    kp = tt([tnx, km], T.prod[:], T.nxi[:], T.m3[:], A.mult)
+    thirds = [T.prod[:, a * M:a * M + M] for a in range(NA)]
+    pT = group([kp], B[0][:, 0:M], [(idb, x) for x in thirds])
+    copy([pL], T.lu[:, 0:MA], B[6][:, 0:MA])
+    kl = copy([], T.lu[:, 2 * MA:MA + M], B[6][:, MA:M])
+    kth = copy([pT], T.th[:], B[0][:, 0:M])
+    halves = (B[1][:, 0:M], B[7][:, 0:M])
+    for h in range(2):
+        for a in range(NA):
+            mm([kcut], halves[h], cut[3 * h], thirds[a], a == 0, False)
+    pAB = []
+    for h in range(2):
+        mm([kth], halves[h], cut[3 * h + 1], T.th[:], False, False)
+        pAB.append(mm([], halves[h], cut[3 * h + 2], T.th[:], False, True))
+    ku0 = copy([], U[0][:], B[0][:, 0:M])
+    kdg = [copy([pAB[h]], T.yd[:, h * M:h * M + M], halves[h]) for h in range(2)]
+    kdig = kdg[1]
+    pun = [unfold([kdg[n // 8]], B[2 + n // 4][:, n % 4 * M:n % 4 * M + M], n, T.yd, M) for n in range(16)]
+    k16 = copy([], T.nx16[:], T.nxi[:])
+    kzx = tsc([kzq], T.zx[:], T.zq[:], head, None, A.mult)
+    knh = copy([k16], T.nxh[:], T.nx16[:])
+    kt0 = []
+    for n in range(16):
+        kt0.append((copy if n // 4 % 2 else act)([pun[n // 4 * 4 + 3]], TD[0][:, n::16], B[2 + n // 4][:, n % 4 * M:n % 4 * M + M]))
+    kn0 = copy([], T.nxu[:], T.nxi[:])
+    kcb = copy([tcap], T.capb[:], T.capf[:])
+    pe = fold([trw[0], trw[1], kl, kzq], B[6][:, 0:2 * M], T.zq, T.rwb, 0, 2 * S)
+
+    def caps(n):
+        return act([trw[n // 2], tcap], T.db[:, n * H:n * H + H], T.rwb[:, n * H:n * H + H], F.Identity, T.capf[:], -1.0)
+
+    def presum(x, deps):
         a, b, c0, c1, c2 = cols(x)
         bank = B[7 if x == 0 else 0][:, 0:c2 - c0]
         mm(deps, bank, idb, T.eo[:, c0:c2], True, False)
@@ -227,16 +251,20 @@ def rank_program(g, core, T, topo):
 
     def places(x, kb, deps):
         a, b, c0, c1, c2 = cols(x)
-        bank = B[1 if x == 0 else 5][:, 0:b - a]
-        mm(deps, bank, idb, T.st16[:, a:b], True, False)
-        mm([kb], bank, T.i1[:], T.bb[:, c0:c1], False, False)
-        p = mm([], bank, T.i1[:], T.bb[:, c1:c2], False, True)
-        return copy([p], T.lu[:, a:b], bank)
+        bank, n = B[1 if x == 0 else 5], b - a
+        mm(deps, bank[:, 0:2 * n], idb, T.st16[:, c0:c2], True, False)
+        mm([], bank[:, n:2 * n], idb, T.row[:, 0:n], False, False)
+        for step, out in ((T.i1, bank[:, 0:n]), (T.i2, bank[:, n:2 * n])):
+            mm([kb], out, step[:], T.bb[:, c0:c1], False, False)
+            p = mm([], out, step[:], T.bb[:, c1:c2], False, step is T.i2)
+        return copy([p], T.lu[:, c0:c2], bank[:, 0:2 * n])
 
-    def tstep(k, h, deps, free):
+    def tstep(k, h, deps, free, later=False):
         a, b = h * H, h * H + H
         t = act(deps, TD[k][:, a:b], TD[k - 1][:].indirect(U[k - 1][:, a // 16:b // 16]))
-        return t, fold([t, kzx] + free, B[h][:, 0:M // 2], T.zx, TD[k], a, b)
+        def into_list():
+            return fold([t, kzx] + free, B[h][:, 0:M // 2], T.zx, TD[k], a, b)
+        return t, into_list if later else into_list()
 
     def tlist(k, h, p):
         return copy([p], U[k][:, h * M // 2:h * M // 2 + M // 2], B[h][:, 0:M // 2])
@@ -244,157 +272,167 @@ def rank_program(g, core, T, topo):
     def rstep(k, a, b, deps):
         return tt(deps, R[k][:, a:b], R[k - 1][:].indirect(U[k - 1][:, a // 16:b // 16]), K[k - 1][:, a:b], A.add)
 
-    pD, ko, kx, kre, xdt = None, None, None, None, []
+    pD, ko, kx, kre = None, None, None, None
     for rnd in range(ROUNDS):
         first, last = rnd == 0, rnd == ROUNDS - 1
         ul, tk, pf_ = {}, {}, {}
+
+        def preload(deps, pieces):
+            for a, b, bank in pieces:
+                mm(deps + [trw[2]], B[bank][:, 0:b - a], idb, T.rwb[:, 2 * S + a:2 * S + b], True, False)
+
         if first:
             ul[0, 0] = ul[0, 1] = ku0
             tk[1, 0], pf_[1, 0] = tstep(1, 0, [ku0] + kt0, [ku0])
+            plo = group([knh] + kt0, B[5][:, 0:288], [(idb, T.nx16[:]), (T.nid[:], T.nxh[:])])
             tk[1, 1], pf_[1, 1] = tstep(1, 1, [], [kdig])
-            ksc = act([psc], T.nsc[:], B[7][:, 0:1])
-            kd = [caps(0)]
-            ra = copy([kl] + trw, R[0][:, 0:SA], T.rwb[:].indirect(T.lu[:, 0:MA]))
-            kc = {(0, 0): dup("G", [ra], 0, 0, XG0)}
-            rb = copy([], R[0][:, SA:S], T.rwb[:].indirect(T.lu[:, MA:M]))
+            psc = group([kcb, kdig], B[7][:, 0:1], [(T.zq[:, 15 - i:143 - i], T.capb[:]) for i in range(16)])
+            klo = act([plo], T.nxl[:], B[5][:, 0:288])
+            wait("Y", *trw)
+            wait("Y", load("Y", "lxd", T.xd[:], T.rw[:]), knh, klo)
+            xdt = [load("Y", "lxh", T.xd[8::16, :], T.nxh[:]), load("Y", "lxl", T.xd[0::16, :], T.nxl[:])]
+            kd = [tsc([trw[0], tcap], T.db[:, 0:CV * H], T.rwb[:, 0:CV * H], -1.0, T.capf[:], A.mult, A.add)] * CV
+            ra = [copy([kl] + trw, R[0][:, 0:SA], T.rwb[:].indirect(T.lu[:, 0:MA]))]
+            kc = {(0, 0): dup("S", ra, 0, 0, XS0)}
+            kd.append(caps(CV))
+            for x in range(2):
+                a0, b0, c0, c1, c2 = cols(x)
+                ke = tsc([pe], T.eo[:, c1:c2], B[6][:, a0:b0], -1.0, None, A.mult)
             ul[1, 0] = tlist(1, 0, pf_[1, 0])
+            for x in range(2):
+                a0, b0, c0, c1, c2 = cols(x)
+                kee = tt([ke], T.eo[:, c0:c1], B[6][:, M + a0:M + b0], T.eo[:, c1:c2], A.add)
+            ke = kee
+            share([ke], T.eo[:], T["ev%d" % rank][:], "ae%d" % rank)
+            rb = copy([], R[0][:, SA:S], T.rwb[:].indirect(T.lu[:, 2 * MA:MA + M]))
             tk[2, 0], pf_[2, 0] = tstep(2, 0, [ul[1, 0], tk[1, 1]], [ul[1, 0]])
-            kv = dup("V", [ra], 0, XG0, SA)
-            free2 = kt0
+            ksc = act([psc], T.nsc[:], B[7][:, 0:1])
+            kv = dup("V", ra, 0, XS0, SA)
         else:
             kla = places(0, choose(0, pD[0]), [ko[0]])
-            ta = act([kla] + xdt, TD[0][:, 0:SA], T.xd[:].indirect(T.lu[:, 0:MA]))
-            ra = copy([kla], R[0][:, 0:SA], T.rwb[:].indirect(T.lu[:, 0:MA]))
-            kc = {(0, 0): dup("G", [ra], 0, 0, XG0)}
+            ta = act([kla] + xdt, TD[0][:, 0:SA], T.xd[:].indirect(T.lu[:, MA:2 * MA]))
+            ra = [copy([kla], R[0][:, 0:SA - R0S], T.rwb[:].indirect(T.lu[:, 0:MA - R0S // 16]))]
+            kc = {(0, 0): dup("G", ra, 0, 0, XG0)}
+            if R0S:
+                ra.append(act([], R[0][:, SA - R0S:SA], T.rwb[:].indirect(T.lu[:, MA - R0S // 16:MA])))
             pD1 = total(rnd - 1, 1, ko[1])
-            kv = dup("V", [ra], 0, XG0, SA)
             kb = choose(1, pD1)
             klb = places(1, kb, [kx[1]])
-            pa_ = fold([ta, ko[1]] + xdt, B[6][:, 0:MA], T.zx, TD[0], 0, SA)
-            tb = act([klb], TD[0][:, SA:S], T.xd[:].indirect(T.lu[:, MA:M]))
-            pb_ = fold([tb], B[7][:, 0:M - MA], T.zx, TD[0], SA, S)
-            rb = copy([klb], R[0][:, SA:S], T.rwb[:].indirect(T.lu[:, MA:M]))
+            kv = dup("S", ra, 0, XG0, SA)
+            pa_ = fold([ta, ko[1]], B[6][:, 0:MA], T.zx, TD[0], 0, SA)
+            tb = act([klb], TD[0][:, SA:S], T.xd[:].indirect(T.lu[:, MA + M:2 * M]))
+            pb_ = fold([tb], B[7][:, 0:MB], T.zx, TD[0], SA, S)
+            rb = copy([klb], R[0][:, SA:S], T.rwb[:].indirect(T.lu[:, 2 * MA:MA + M]))
             ul[0, 0] = copy([pa_], U[0][:, 0:MA], B[6][:, 0:MA])
             tk[0, 1] = tb
-            free2 = kre + xdt
+        preload(kt0 if first else kre, PIECES[:3])
         kc[0, 0] += kv
-        kc[0, 1] = kv + dup("G", [rb], 0, SA, S)
-        kr = rb
-        for a in range(3):
-            mm(free2 + [trw[2]], B[2 + a][:], idb, T.rwb[:, 2 * S + 512 * a:2 * S + 512 * a + 512], True, False)
+        xg = 0 if first else XG1
+        kc[0, 1] = kv + dup("G", [rb], 0, SA, SA + xg) + dup("V", [rb], 0, SA + xg, S)
+        kr = [rb] + ra
         for k in (1, 2, 3):
             for h in range(2):
                 a = h * H
-                lo = a if k < 3 or h else RS
+                lo = max(a, RS) if k == 3 else a
+                hi = min(a + H, S - RT) if k == 3 else a + H
                 if not first:
-                    tk[k, h], pf_[k, h] = tstep(k, h, [ul[k - 1, h], tk[k - 1, 1]], [ul[k - 1, h], kb])
-                r = rstep(k, a, a + H, [kr, ul[k - 1, h]] + kc[k - 1, h])
+                    tk[k, h], pf_[k, h] = tstep(k, h, [ul[k - 1, h], tk[k - 1, 1]], [ul[k - 1, h], kb], (k, h) == (3, 1))
+                r = rstep(k, a, a + H, kr + [ul[k - 1, h]] + kc[k - 1, h])
                 if h:
-                    kr = r
-                xg = 0 if first and k > EAT else XG
-                xs = 0 if first else XS
-                kc[k, h] = dup("G", [r], k, lo, min(lo + xg, a + H))
-                kc[k, h] += dup("S", [r], k, lo + xg, min(lo + xg + xs, a + H))
+                    kr = [r]
+                xg = 0 if first and k < GK else XG3 if k == 3 else XG
+                xs = min(XS1[k - 1], hi - lo - xg) if first else 0 if k == 3 else XS
+                kc[k, h] = dup("G", [r], k, lo, lo + xg) + dup("S", [r], k, lo + xg, lo + xg + xs)
                 if first:
-                    if (k, h) == (EAT, 1):
-                        share([ke], T.eo[:], T["ev%d" % rank][:], "ae%d" % rank)
                     kt, ht = {(1, 0): (1, 1), (1, 1): (2, 0), (2, 1): (2, 1), (3, 0): (3, 0)}.get((k, h), (0, 0))
                     if kt:
                         ul[kt, ht] = tlist(kt, ht, pf_[kt, ht])
                     if 0 < kt < 3:
-                        kd.append(caps(len(kd)))
+                        if len(kd) < 4:
+                            kd.append(caps(len(kd)))
                         tk[kt + 1, ht], pf_[kt + 1, ht] = tstep(kt + 1, ht, [ul[kt, ht], tk[kt, 1]], [ul[kt, ht]])
-                    if (k, h) == (1, 0):
-                        for x in range(2):
-                            a0, b0, c0, c1, c2 = cols(x)
-                            ke = tsc([pe], T.eo[:, c1:c2], B[6][:, a0:b0], -1.0, None, A.mult)
-                        for x in range(2):
-                            a0, b0, c0, c1, c2 = cols(x)
-                            ke = tt([ke], T.eo[:, c0:c1], B[6][:, M + a0:M + b0], T.eo[:, c1:c2], A.add)
                 elif h == 0:
-                    ul[k - 1, 1] = copy([pb_], U[0][:, MA:M], B[7][:, 0:M - MA]) if k == 1 else tlist(k - 1, 1, pf_[k - 1, 1])
+                    ul[k - 1, 1] = copy([pb_], U[0][:, MA:M], B[7][:, 0:MB]) if k == 1 else tlist(k - 1, 1, pf_[k - 1, 1])
                 else:
                     ul[k, 0] = tlist(k, 0, pf_[k, 0])
-                kc[k, h] += dup("V", [r], k, lo + xg + xs, a + H)
-        mm([kr] + kt0 + ([] if first else [klb]), B[5][:, 0:RS], idb, R[3][:, 0:RS], True, False)
-        hz = act([kr, ul[3, 0]], T.zr[:], R[3][:].indirect(U[3][:, 0:RS // 16]))
-        pz = mm([hz], B[5][:, 0:RS], idb, T.zr[:], False, True)
-        ks = act([pz], R[4][:, 0:RS], B[5][:, 0:RS])
-        rstep(4, RS, H, [kr, ul[3, 0]] + kc[3, 0])
+                kc[k, h] += dup("V", [r], k, lo + xg + xs, hi)
+        ends = ((0, RS, B[5], [klo if first else klb]), (S - RT, S, B[7], [ksc, ul[0, 1]]))
+        for a, b, bank, deps in ends:
+            mm(kr + deps, bank[:, 0:b - a], idb, R[3][:, a:b], True, False)
+        if not first:
+            pf_[3, 1] = pf_[3, 1]()
+        rstep(4, RS, H, kr + [ul[3, 0]] + kc[3, 0])
         ul[3, 1] = tlist(3, 1, pf_[3, 1])
-        kv = rstep(4, H, S, [ul[3, 1]] + kc[3, 1])
+        kv = rstep(4, H, S - RT, [ul[3, 1]] + kc[3, 1])
+        pz = []
+        for n, (a, b, bank, deps) in enumerate(ends):
+            hz = act(kr + [ul[3, n]], T.zr[:, a:b], R[3][:].indirect(U[3][:, a // 16:b // 16]))
+            pz.append(mm([hz], bank[:, 0:b - a], idb, T.zr[:, a:b], False, True))
+        for n, (a, b, bank, deps) in enumerate(ends):
+            ks = act([pz[n]], R[4][:, a:b], bank[:, 0:b - a])
         o = T["o%d" % rnd]
 
         def vsum(a, x, deps):
             a0, b0 = BLK[x]
-            return tt(deps, T["tv%d" % a][:, 16 * a0:16 * b0], R[4][:].indirect(T.nxu[:, a * M + a0:a * M + b0]),
-                      T.db[:, a * S + 16 * a0:a * S + 16 * b0], A.min)
+            out = (T.qs[:, S:S + SB] if x else T.qs[:, S + SB:2 * S]) if a else T.tv0[:, 16 * a0:16 * b0]
+            return tt(deps, out, R[4][:].indirect(T.nxu[:, a * M + a0:a * M + b0]), T.db[:, a * S + 16 * a0:a * S + 16 * b0], A.min)
 
         def sgather(n):
-            z = act([kv, ks, kn0], T.zs[:, 512 * n:512 * n + 512], R[4][:].indirect(T.nxu[:, 2 * M + 32 * n:2 * M + 32 * n + 32]))
-            return mm([z], B[2 + n][:], idb, T.zs[:, 512 * n:512 * n + 512], False, True)
+            a, b, bank = PIECES[n]
+            z = act([kv, ks, kn0], T.zs[:, a:b], R[4][:].indirect(T.nxu[:, 2 * M + a // 16:2 * M + b // 16]))
+            return lambda: mm([z], B[bank][:, 0:b - a], idb, T.zs[:, a:b], False, True)
 
         def srelu(n, p):
-            return act([p], T.ts[:, 512 * n:512 * n + 512], B[2 + n][:], F.Relu, T.capf[:], -1.0)
+            a, b, bank = PIECES[n]
+            return act([p], T.qs[:, a:b], B[bank][:, 0:b - a], F.Relu, T.capf[:], -1.0)
 
-        def base(x, p, bank):
+        def base(x, p, q0):
             a0, b0, c0, c1, c2 = cols(x)
-            act([p], T.x0[:, c0:c1], bank[:, 0:b0 - a0])
-            return act([ksc], T.x0[:, c1:c2], bank[:, 0:b0 - a0], F.Identity, T.nsc[:], -1.0)
+            act([p], T.x0[:, c0:c1], q0)
+            return act([ksc], T.x0[:, c1:c2], q0, F.Identity, T.nsc[:], -1.0)
 
-        def differ(x, kx0, pp_, p1, bank):
+        def differ(x, deps2, q2, deps1, q1):
             a0, b0, c0, c1, c2 = cols(x)
-            n = b0 - a0
-            tt([kx0, pp_, p1], o[:, c1:c2], T.x0[:, c1:c2], bank[:, n:2 * n], A.subtract)
-            k = tt([], o[:, c0:c1], bank[:, 0:n], T.x0[:, c0:c1], A.subtract)
+            tt(deps2, o[:, c1:c2], T.x0[:, c1:c2], q2, A.subtract)
+            k = tt(deps1, o[:, c0:c1], q1, T.x0[:, c0:c1], A.subtract)
             share([k], o[:, c0:c2], T["v%d_%d" % (rnd, rank)][:, c0:c2], "a%d_%d_%d" % (rnd, x, rank))
             return k
 
+        preload([ks], PIECES[3:])
         h0a = vsum(0, 0, [kv, ks] + kd)
         h1a = vsum(1, 0, [])
         h0b = vsum(0, 1, [])
-        z = [sgather(0), sgather(1)]
+        z = [sgather(0)(), sgather(1)()]
         kre = [srelu(0, z[0]), srelu(1, z[1])]
+        late = range(2, len(PIECES))
         p0a = fold([h0a, kzq, ul[3, 0]], B[0][:, 0:MA], T.zq, T.tv0, 0, SA)
-        ppa = fold([kre[1], ul[3, 1]], B[1][:, MA:2 * MA], T.zq, T.ts, 0, SA)
-        p1a = fold([h1a], B[1][:, 0:MA], T.zq, T.tv1, 0, SA)
-        kx = [base(0, p0a, B[0])]
-        z2 = sgather(2)
-        kre.append(srelu(2, z2))
-        ko = [differ(0, kx[0], ppa, p1a, B[1])]
-        h1b = vsum(1, 1, [])
-        p0b = fold([h0b, ks], B[5][:, 0:M - MA], T.zq, T.tv0, SA, S)
-        ppb = fold([kre[2], ke, ul[0, 0]], B[6][:, M - MA:2 * (M - MA)], T.zq, T.ts, SA, S)
-        p1b = fold([h1b], B[6][:, 0:M - MA], T.zq, T.tv1, SA, S)
-        kx.append(base(1, p0b, B[5]))
-        ko.append(differ(1, kx[1], ppb, p1b, B[6]))
-        if not first:
-            presum(rnd, 0, [ke, ksc, ul[0, 1]])
-            presum(rnd, 1, [kx[0]])
-        if first:
-            t16 = copy([], T.nx16[:], T.nxi[:])
-            pA = group([t16] + kre, B[2][:, 0:288], [(T.pa[:], T.nx16[:])])
-            pB = group([], B[3][:, 0:288], [(T.pb[:], T.nx16[:])])
-            dig = [digits([p], B[2 + h][:, 0:288], T.xt[:, 288 * h:288 * h + 288], T.xs[:, 288 * h:288 * h + 288],
-                          T.xb[:, 288 * h:288 * h + 288]) for h, p in enumerate((pA, pB))]
-            free = {4: [], 6: [ko[1]], 2: [dig[0]], 3: [dig[1]]}
-            for n in range(16):
-                h, j = n // 8, n % 8
-                b = (4, 6, 2)[n % 3] if n < 6 else (4, 6, 2, 3)[(n - 6) % 4]
-                if n == 4:
-                    presum(rnd, 0, [ke, ksc, ul[0, 1]])
-                    presum(rnd, 1, [kx[0]])
-                if n == 12:
-                    pD = [total(rnd, 0, ko[0])]
-                tok = group([dig[h]] + free[b], B[b][:, 0:288], [(T.idz[:, j:j + 128], T.xb[:, 288 * h:288 * h + 288])])
-                mine = n >= 16 - 2 * XDV and n % 2 == 0
-                free[b] = [(copy if mine else act)([tok], T.xd[:, n::16], B[b][:, 0:288])]
-                xdt += free[b]
-        else:
-            pD = [total(rnd, 0, ko[0])]
+        ppa = fold([kre[1], ul[3, 1]], B[1][:, MA:2 * MA], T.zq, T.qs, 0, SA)
+        if OPT["z2"]:
+            adds = [sgather(n) for n in late]
+        kx = [base(0, p0a, B[0][:, 0:MA])]
+        if not OPT["z2"]:
+            adds = [sgather(n) for n in late]
+        if OPT["add2"]:
+            z = [f() for f in adds]
+        p1a = fold([h1a], B[1][:, 0:MA], T.zq, T.qs, S + SB, 2 * S)
+        if not OPT["add2"]:
+            z = [f() for f in adds]
+        kre += [srelu(n, z[n - 2]) for n in late]
+        if OPT["sub"]:
+            h1b = vsum(1, 1, [])
+        ko = [differ(0, [kx[0], p1a], B[1][:, MA:2 * MA], [], B[1][:, 0:MA])]
+        if not OPT["sub"]:
+            h1b = vsum(1, 1, [])
+        p0b = fold([h0b, ks], B[5][:, 0:MB], T.zq, T.tv0, SA, S)
+        p1b = fold([h1b, kre[-1], ke, ul[0, 0]], B[6][:, 0:2 * MB], T.zq, T.qs, SA, S + SB)
+        kx.append(base(1, p0b, B[5][:, 0:MB]))
+        ko.append(differ(1, [kx[1], p1b], B[6][:, 0:MB], [], B[6][:, MB:2 * MB]))
+        presum(0, [ke, kre[-1]])
+        presum(1, [kx[0]])
+        pD = [total(rnd, 0, ko[0])]
         if last:
             ky = tsc([kv, ks, tcap], T.yb[:], R[4][:], T.capf[:], None, A.min)
-            wait("Y", ky)
+            wait("Y", ky, ("loc", sent[0]))
             sy = load("Y", "st0", T.yr[:], T.yb[:])
     for x in range(2):
         a, b, c0, c1, c2 = cols(x)

from concourse.bass import DstId, RemoteDMATransfer
from concourse.mybir import AluOpType as A, ActivationFunctionType as F

NR, ROUNDS = 8, 3
S, NA = 1536, 3
M = S // 16
H = S // 2
MA = 56
SA, MB = 16 * MA, M - MA
SB = S - SA
BLK = ((0, MA), (MA, M))
PIECES = ((0, SA // 2, 2), (SA // 2, SA, 3), (SA, min(SA + 512, S), 4), (SA + 512, S, 7))[:3 if SB <= 512 else 4]
OPT = dict(z2=0, add2=0, sub=0)
XG, XS = 448, 160
XG3 = 384
XG0, XG1 = 512, 448
R0S = 224
RS, RT = 256, 192
GK = 3
XS0, XS1 = 512, (384, 512, 320)
CV = 2

_B, _H, _F, _I, _U = "bfloat16", "float16", "float32", "int32", "uint16"
SCRATCH = {
    "nxi": ("sbuf", [128, 288], _I), "acti": ("sbuf", [128, 96], _I), "capf": ("sbuf", [128, 1], _F),
    "rwb": ("sbuf", [128, 4608], _B), "db": ("sbuf", [128, 2 * S], _B), "xd": ("sbuf", [128, 4608], _B),
    "nx16": ("sbuf", [128, 288], _H), "nxh": ("sbuf", [128, 288], _B), "nxu": ("sbuf", [128, 288], _U),
    "m3": ("sbuf", [128, 288], _H), "prod": ("sbuf", [128, 288], _H), "act16": ("sbuf", [128, 96], _B),
    "nxl": ("sbuf", [128, 288], _B), "th": ("sbuf", [128, 96], _B), "yd": ("sbuf", [128, 192], _B),
    "lu": ("sbuf", [128, 192], _U), "sti": ("sbuf", [128, 192], _I), "pi": ("sbuf", [128, 1], _I),
    "pm": ("sbuf", [128, 12], _I), "pc": ("sbuf", [128, 20], _F),
    "nid": ("sbuf", [128, 128], _B), "i2": ("sbuf", [128, 128], _B), "row": ("sbuf", [128, 64], _H),
    "st16": ("sbuf", [128, 192], _H), "capb": ("sbuf", [128, 1], _B), "nsc": ("sbuf", [128, 1], _F),
    "bb": ("sbuf", [128, 192], _H), "wm": ("sbuf", [128, 192], _F),
    "zr": ("sbuf", [128, S], _B), "qs": ("sbuf", [128, 2 * S], _B), "tv0": ("sbuf", [128, S], _B), "zs": ("sbuf", [128, S], _B),
    "x0": ("sbuf", [128, 192], _F), "eo": ("sbuf", [128, 192], _H),
    "yb": ("sbuf", [128, S], _B), "yf": ("sbuf", [128, 96], _F),
    "cut": ("sbuf", [128, 768], _B), "idz": ("sbuf", [128, 144], _B), "i1": ("sbuf", [128, 128], _B),
    "zx": ("sbuf", [128, 144], _B), "zq": ("sbuf", [128, 144], _B),
}
for _k in range(5):
    SCRATCH["r%d" % _k] = ("sbuf", [128, S], _B)
for _k in range(4):
    SCRATCH["k%d" % _k] = ("sbuf", [128, S], _B)
    SCRATCH["t%d" % _k] = ("sbuf", [128, S], _B)
    SCRATCH["u%d" % _k] = ("sbuf", [128, 96], _U)
for _k in range(8):
    SCRATCH["b%d" % _k] = ("psum", [128, 512], _F)
    SCRATCH["ev%d" % _k] = ("sbuf", [128, 192], _H)
for _r in range(ROUNDS):
    SCRATCH["o%d" % _r] = ("sbuf", [128, 192], _H)
    for _k in range(NR):
        SCRATCH["v%d_%d" % (_r, _k)] = ("sbuf", [128, 192], _H)
SEMAPHORES = ["cV", "cS", "cP", "cG", "lnx", "lact", "lcap", "lrw0", "lrw1", "lrw2", "st0", "st1", "loc", "lxd", "lxh", "lxl"]
SEMAPHORES += ["ae%d" % k for k in range(NR)]
SEMAPHORES += ["a%d_%d_%d" % (r, x, k) for r in range(ROUNDS) for x in range(2) for k in range(NR)]


def rank_program(g, core, T, topo):
    rank = T.rank_of(core)
    if rank is None:
        return
    queue = {"V": g.vector, "S": g.scalar, "P": g.tensor, "G": g, "Y": g.sync}
    V, SC, PE = g.vector, g.scalar, g.tensor
    count = {"V": 0, "S": 0, "P": 0, "G": 0}
    seen = {}
    B = [T["b%d" % n] for n in range(8)]
    R, K, TD, U = ([T["%s%d" % (c, n)] for n in range(k)] for c, k in (("r", 5), ("k", 4), ("t", 4), ("u", 4)))
    idb = T.idz[:, 8:136]

    def wait(q, *toks):
        for name, val in toks:
            if seen.get((q, name), 0) < val:
                queue[q].wait_ge(T.sem[name], val)
                seen[(q, name)] = val

    def mark(q, ins):
        count[q] += 1
        ins.then_inc(T.sem["c" + q], 1)
        return ("c" + q, count[q])

    def load(q, name, out, in_):
        queue[q].dma_start(out, in_).then_inc(T.sem[name], 16)
        return (name, 16)

    def copy(deps, out, in_):
        wait("V", *deps)
        return mark("V", V.tensor_copy(out, in_))

    def tt(deps, out, a, b, op):
        wait("V", *deps)
        return mark("V", V.tensor_tensor(out, a, b, op))

    def tsc(deps, out, a, s1, s2, op0, op1=None):
        wait("V", *deps)
        if op1 is None:
            return mark("V", V.tensor_scalar(out, a, s1, None, op0))
        return mark("V", V.tensor_scalar(out, a, s1, s2, op0, op1))

    def act(deps, out, in_, func=F.Copy, *more):
        wait("S", *deps)
        return mark("S", SC.activation(out, in_, func, *more))

    def mm(deps, out, lhsT, rhs, start, stop):
        wait("P", *deps)
        ins = PE.matmul(out, lhsT, rhs, start, stop)
        return mark("P", ins) if stop else None

    def group(deps, out, pairs):
        wait("P", *deps)
        tok = None
        for n, (l, r) in enumerate(pairs):
            tok = mm([], out, l, r, n == 0, n == len(pairs) - 1)
        return tok

    def fold(deps, out, z, buf, a, b):
        return group(deps, out, [(z[:, 15 - i:143 - i], buf[:, a + i:b:16]) for i in range(16)])

    def pick(tok, name, pattern, op, fill, base, cm):
        wait("G", tok)
        return mark("G", g.affine_select(T[name][:], T[name][:], pattern, op, fill, base, cm))

    def dup(q, deps, k, a, b):
        if a >= b:
            return []
        if q == "V":
            return [copy(deps, K[k][:, a:b], R[k][:, a:b])]
        if q == "S":
            return [act(deps, K[k][:, a:b], R[k][:, a:b])]
        wait("G", *deps)
        return [mark("G", g.affine_select(K[k][:, a:b], R[k][:, a:b], [[0, b - a]], A.is_ge, 0.0, 0, 0))]

    others = [T.cores[(rank + n) % NR] for n in range(1, NR)]
    before = [(rank - n) % NR for n in range(1, NR)]
    sent = [0]

    def share(deps, src, land, sem):
        wait("G", *deps)
        mask = topo.mask(core, others[0])
        ids = []
        for d in others:
            mask &= topo.mask(core, d)
            rid, pid = topo.addr(d, core)
            ids.append(DstId(rid=rid, pnc=pid))
        g.remote_dma_fused([RemoteDMATransfer(dst_ids=ids, dma_engine_mask=mask, remote_sem=T.sem[sem], srcs=[src],
                                              dsts=[land for d in others])], local_sem=T.sem["loc"])
        sent[0] += len([n for n in range(16) if mask >> n & 1])

    arrival = len(topo.engines(others[0], core))

    tnx = load("Y", "lnx", T.nxi[:], T.nx[:])
    tact = load("S", "lact", T.acti[:], T.act0[:])
    tcap = load("S", "lcap", T.capf[:], T.cap[:])
    trw = [load("Y", "lrw%d" % a, T.rwb[:, a * S:(a + 1) * S], T.rw[:, a * S:(a + 1) * S]) for a in range(NA)]

    def cols(x):
        a, b = BLK[x]
        return a, b, 2 * a, a + b, 2 * b

    kz = mark("V", V.memset(T.idz[:], 0.0))
    kq = mark("V", V.memset(T.zq[:], 1.0))
    kpi = mark("G", g.iota(T.pi[:], [[1, 1]], 0, 1))
    kid = pick(kz, "idz", [[-1, 144]], A.not_equal, 1.0, 8, 1)
    mark("G", g.iota(T.sti[:, 0:M], [[16, M]], 0, 0))
    ksti = mark("G", g.iota(T.sti[:, M:2 * M], [[1, M]], 0, 0))
    k = pick(kq, "zq", [[0, 9], [1, 16]], A.is_ge, 0.0, -15, 0)
    k = pick(k, "zq", [[-16, 9], [0, 16]], A.is_ge, 0.0, 0, 1)
    kzq = pick(k, "zq", [[16, 9], [0, 16]], A.is_ge, 0.0, 15, -1)
    for n, bits in enumerate((15, 8, 7)):
        k = tsc([kpi], T.pm[:, 4 * n:4 * n + 1], T.pi[:], bits, None, A.bitwise_and)
    p16, low, high, head = (T.pc[:, 4 * n:4 * n + 1] for n in range(4))
    copy([k], p16, T.pm[:, 0:1])
    tsc([], low, T.pm[:, 4:5], 0.0, None, A.is_equal)
    tsc([], high, T.pm[:, 4:5], 8.0, None, A.is_equal)
    kpc = tsc([], head, T.pm[:, 8:9], 0.0, None, A.is_equal)
    cut = [T.cut[:, 128 * n:128 * n + 128] for n in range(6)]
    for n, (c, half, sign) in enumerate(((8, low, 1.0), (8, low, -1.0), (0, low, 1.0), (16, high, 1.0), (16, high, -1.0), (8, high, 1.0))):
        kcut = tsc([kid, kpc], cut[n], T.idz[:, c:c + 128], half, sign, A.mult, A.mult)
    tsc([], T.i1[:], idb, float(S), None, A.mult)
    tsc([], T.i2[:], idb, float(M), None, A.mult)
    tsc([], T.nid[:], idb, -1.0, None, A.mult)
    k = tsc([], T.pc[:, 16:17], p16, 288.0, None, A.mult)
    for x in range(2):
        a, b, c0, c1, c2 = cols(x)
        tsc([ksti], T.st16[:, c0:c1], T.sti[:, a:b], p16, None, A.add)
        copy([], T.st16[:, c1:c2], T.sti[:, M + a:M + b])
    kst = tsc([k], T.row[:], T.sti[:, 0:64], 0.0, T.pc[:, 16:17], A.mult, A.add)

    def unfold(deps, out, n, src, width):
        j = n % 8
        return group(deps, out, [(T.idz[:, 8 + j:136 + j], src[:, n // 8 * width:n // 8 * width + width])])

    for a in range(NA):
        km = tsc([tact], T.m3[:, a * M:a * M + M], T.acti[:], float(a), None, A.is_equal)
    ka16 = copy([], T.act16[:], T.acti[:])
    for x in range(2):
        a, b, c0, c1, c2 = cols(x)
        pL = group([kst, ka16], B[6][:, a:b], [(T.i1[:], T.act16[:, a:b]), (idb, T.st16[:, c0:c1])])
    kp = tt([tnx, km], T.prod[:], T.nxi[:], T.m3[:], A.mult)
    thirds = [T.prod[:, a * M:a * M + M] for a in range(NA)]
    pT = group([kp], B[0][:, 0:M], [(idb, x) for x in thirds])
    copy([pL], T.lu[:, 0:MA], B[6][:, 0:MA])
    kl = copy([], T.lu[:, 2 * MA:MA + M], B[6][:, MA:M])
    kth = copy([pT], T.th[:], B[0][:, 0:M])
    halves = (B[1][:, 0:M], B[7][:, 0:M])
    for h in range(2):
        for a in range(NA):
            mm([kcut], halves[h], cut[3 * h], thirds[a], a == 0, False)
    pAB = []
    for h in range(2):
        mm([kth], halves[h], cut[3 * h + 1], T.th[:], False, False)
        pAB.append(mm([], halves[h], cut[3 * h + 2], T.th[:], False, True))
    ku0 = copy([], U[0][:], B[0][:, 0:M])
    kdg = [copy([pAB[h]], T.yd[:, h * M:h * M + M], halves[h]) for h in range(2)]
    kdig = kdg[1]
    pun = [unfold([kdg[n // 8]], B[2 + n // 4][:, n % 4 * M:n % 4 * M + M], n, T.yd, M) for n in range(16)]
    k16 = copy([], T.nx16[:], T.nxi[:])
    kzx = tsc([kzq], T.zx[:], T.zq[:], head, None, A.mult)
    knh = copy([k16], T.nxh[:], T.nx16[:])
    kt0 = []
    for n in range(16):
        kt0.append((copy if n // 4 % 2 else act)([pun[n // 4 * 4 + 3]], TD[0][:, n::16], B[2 + n // 4][:, n % 4 * M:n % 4 * M + M]))
    kn0 = copy([], T.nxu[:], T.nxi[:])
    kcb = copy([tcap], T.capb[:], T.capf[:])
    pe = fold([trw[0], trw[1], kl, kzq], B[6][:, 0:2 * M], T.zq, T.rwb, 0, 2 * S)

    def caps(n):
        return act([trw[n // 2], tcap], T.db[:, n * H:n * H + H], T.rwb[:, n * H:n * H + H], F.Identity, T.capf[:], -1.0)

    def presum(x, deps):
        a, b, c0, c1, c2 = cols(x)
        bank = B[7 if x == 0 else 0][:, 0:c2 - c0]
        mm(deps, bank, idb, T.eo[:, c0:c2], True, False)
        for p in before:
            mm([("ae%d" % p, arrival)], bank, idb, T["ev%d" % p][:, c0:c2], False, False)

    def total(rnd, x, ko):
        a, b, c0, c1, c2 = cols(x)
        bank = B[7 if x == 0 else 0][:, 0:c2 - c0]
        mm([ko], bank, idb, T["o%d" % rnd][:, c0:c2], False, False)
        for n, p in enumerate(before):
            k = mm([("a%d_%d_%d" % (rnd, x, p), arrival)], bank, idb, T["v%d_%d" % (rnd, p)][:, c0:c2], False, n == NR - 2)
        return k

    def choose(x, pD):
        a, b, c0, c1, c2 = cols(x)
        bank, n = B[7 if x == 0 else 0], b - a
        tsc([pD], T.wm[:, c0:c1], bank[:, n:2 * n], -40000.0, 0.0, A.mult, A.min)
        kw = tsc([], T.wm[:, c1:c2], bank[:, 0:n], 0.0, None, A.max)
        return tt([kw], T.bb[:, c0:c2], bank[:, 0:2 * n], T.wm[:, c0:c2], A.is_gt)

    def places(x, kb, deps):
        a, b, c0, c1, c2 = cols(x)
        bank, n = B[1 if x == 0 else 5], b - a
        mm(deps, bank[:, 0:2 * n], idb, T.st16[:, c0:c2], True, False)
        mm([], bank[:, n:2 * n], idb, T.row[:, 0:n], False, False)
        for step, out in ((T.i1, bank[:, 0:n]), (T.i2, bank[:, n:2 * n])):
            mm([kb], out, step[:], T.bb[:, c0:c1], False, False)
            p = mm([], out, step[:], T.bb[:, c1:c2], False, step is T.i2)
        return copy([p], T.lu[:, c0:c2], bank[:, 0:2 * n])

    def tstep(k, h, deps, free, later=False):
        a, b = h * H, h * H + H
        t = act(deps, TD[k][:, a:b], TD[k - 1][:].indirect(U[k - 1][:, a // 16:b // 16]))
        def into_list():
            return fold([t, kzx] + free, B[h][:, 0:M // 2], T.zx, TD[k], a, b)
        return t, into_list if later else into_list()

    def tlist(k, h, p):
        return copy([p], U[k][:, h * M // 2:h * M // 2 + M // 2], B[h][:, 0:M // 2])

    def rstep(k, a, b, deps):
        return tt(deps, R[k][:, a:b], R[k - 1][:].indirect(U[k - 1][:, a // 16:b // 16]), K[k - 1][:, a:b], A.add)

    pD, ko, kx, kre = None, None, None, None
    for rnd in range(ROUNDS):
        first, last = rnd == 0, rnd == ROUNDS - 1
        ul, tk, pf_ = {}, {}, {}

        def preload(deps, pieces):
            for a, b, bank in pieces:
                mm(deps + [trw[2]], B[bank][:, 0:b - a], idb, T.rwb[:, 2 * S + a:2 * S + b], True, False)

        if first:
            ul[0, 0] = ul[0, 1] = ku0
            tk[1, 0], pf_[1, 0] = tstep(1, 0, [ku0] + kt0, [ku0])
            plo = group([knh] + kt0, B[5][:, 0:288], [(idb, T.nx16[:]), (T.nid[:], T.nxh[:])])
            tk[1, 1], pf_[1, 1] = tstep(1, 1, [], [kdig])
            psc = group([kcb, kdig], B[7][:, 0:1], [(T.zq[:, 15 - i:143 - i], T.capb[:]) for i in range(16)])
            klo = act([plo], T.nxl[:], B[5][:, 0:288])
            wait("Y", *trw)
            wait("Y", load("Y", "lxd", T.xd[:], T.rw[:]), knh, klo)
            xdt = [load("Y", "lxh", T.xd[8::16, :], T.nxh[:]), load("Y", "lxl", T.xd[0::16, :], T.nxl[:])]
            kd = [tsc([trw[0], tcap], T.db[:, 0:CV * H], T.rwb[:, 0:CV * H], -1.0, T.capf[:], A.mult, A.add)] * CV
            ra = [copy([kl] + trw, R[0][:, 0:SA], T.rwb[:].indirect(T.lu[:, 0:MA]))]
            kc = {(0, 0): dup("S", ra, 0, 0, XS0)}
            kd.append(caps(CV))
            for x in range(2):
                a0, b0, c0, c1, c2 = cols(x)
                ke = tsc([pe], T.eo[:, c1:c2], B[6][:, a0:b0], -1.0, None, A.mult)
            ul[1, 0] = tlist(1, 0, pf_[1, 0])
            for x in range(2):
                a0, b0, c0, c1, c2 = cols(x)
                kee = tt([ke], T.eo[:, c0:c1], B[6][:, M + a0:M + b0], T.eo[:, c1:c2], A.add)
            ke = kee
            share([ke], T.eo[:], T["ev%d" % rank][:], "ae%d" % rank)
            rb = copy([], R[0][:, SA:S], T.rwb[:].indirect(T.lu[:, 2 * MA:MA + M]))
            tk[2, 0], pf_[2, 0] = tstep(2, 0, [ul[1, 0], tk[1, 1]], [ul[1, 0]])
            ksc = act([psc], T.nsc[:], B[7][:, 0:1])
            kv = dup("V", ra, 0, XS0, SA)
        else:
            kla = places(0, choose(0, pD[0]), [ko[0]])
            ta = act([kla] + xdt, TD[0][:, 0:SA], T.xd[:].indirect(T.lu[:, MA:2 * MA]))
            ra = [copy([kla], R[0][:, 0:SA - R0S], T.rwb[:].indirect(T.lu[:, 0:MA - R0S // 16]))]
            kc = {(0, 0): dup("G", ra, 0, 0, XG0)}
            if R0S:
                ra.append(act([], R[0][:, SA - R0S:SA], T.rwb[:].indirect(T.lu[:, MA - R0S // 16:MA])))
            pD1 = total(rnd - 1, 1, ko[1])
            kb = choose(1, pD1)
            klb = places(1, kb, [kx[1]])
            kv = dup("S", ra, 0, XG0, SA)
            pa_ = fold([ta, ko[1]], B[6][:, 0:MA], T.zx, TD[0], 0, SA)
            tb = act([klb], TD[0][:, SA:S], T.xd[:].indirect(T.lu[:, MA + M:2 * M]))
            pb_ = fold([tb], B[7][:, 0:MB], T.zx, TD[0], SA, S)
            rb = copy([klb], R[0][:, SA:S], T.rwb[:].indirect(T.lu[:, 2 * MA:MA + M]))
            ul[0, 0] = copy([pa_], U[0][:, 0:MA], B[6][:, 0:MA])
            tk[0, 1] = tb
        preload(kt0 if first else kre, PIECES[:3])
        kc[0, 0] += kv
        xg = 0 if first else XG1
        kc[0, 1] = kv + dup("G", [rb], 0, SA, SA + xg) + dup("V", [rb], 0, SA + xg, S)
        kr = [rb] + ra
        for k in (1, 2, 3):
            for h in range(2):
                a = h * H
                lo = max(a, RS) if k == 3 else a
                hi = min(a + H, S - RT) if k == 3 else a + H
                if not first:
                    tk[k, h], pf_[k, h] = tstep(k, h, [ul[k - 1, h], tk[k - 1, 1]], [ul[k - 1, h], kb], (k, h) == (3, 1))
                r = rstep(k, a, a + H, kr + [ul[k - 1, h]] + kc[k - 1, h])
                if h:
                    kr = [r]
                xg = 0 if first and k < GK else XG3 if k == 3 else XG
                xs = min(XS1[k - 1], hi - lo - xg) if first else 0 if k == 3 else XS
                kc[k, h] = dup("G", [r], k, lo, lo + xg) + dup("S", [r], k, lo + xg, lo + xg + xs)
                if first:
                    kt, ht = {(1, 0): (1, 1), (1, 1): (2, 0), (2, 1): (2, 1), (3, 0): (3, 0)}.get((k, h), (0, 0))
                    if kt:
                        ul[kt, ht] = tlist(kt, ht, pf_[kt, ht])
                    if 0 < kt < 3:
                        if len(kd) < 4:
                            kd.append(caps(len(kd)))
                        tk[kt + 1, ht], pf_[kt + 1, ht] = tstep(kt + 1, ht, [ul[kt, ht], tk[kt, 1]], [ul[kt, ht]])
                elif h == 0:
                    ul[k - 1, 1] = copy([pb_], U[0][:, MA:M], B[7][:, 0:MB]) if k == 1 else tlist(k - 1, 1, pf_[k - 1, 1])
                else:
                    ul[k, 0] = tlist(k, 0, pf_[k, 0])
                kc[k, h] += dup("V", [r], k, lo + xg + xs, hi)
        ends = ((0, RS, B[5], [klo if first else klb]), (S - RT, S, B[7], [ksc, ul[0, 1]]))
        for a, b, bank, deps in ends:
            mm(kr + deps, bank[:, 0:b - a], idb, R[3][:, a:b], True, False)
        if not first:
            pf_[3, 1] = pf_[3, 1]()
        rstep(4, RS, H, kr + [ul[3, 0]] + kc[3, 0])
        ul[3, 1] = tlist(3, 1, pf_[3, 1])
        kv = rstep(4, H, S - RT, [ul[3, 1]] + kc[3, 1])
        pz = []
        for n, (a, b, bank, deps) in enumerate(ends):
            hz = act(kr + [ul[3, n]], T.zr[:, a:b], R[3][:].indirect(U[3][:, a // 16:b // 16]))
            pz.append(mm([hz], bank[:, 0:b - a], idb, T.zr[:, a:b], False, True))
        for n, (a, b, bank, deps) in enumerate(ends):
            ks = act([pz[n]], R[4][:, a:b], bank[:, 0:b - a])
        o = T["o%d" % rnd]

        def vsum(a, x, deps):
            a0, b0 = BLK[x]
            out = (T.qs[:, S:S + SB] if x else T.qs[:, S + SB:2 * S]) if a else T.tv0[:, 16 * a0:16 * b0]
            return tt(deps, out, R[4][:].indirect(T.nxu[:, a * M + a0:a * M + b0]), T.db[:, a * S + 16 * a0:a * S + 16 * b0], A.min)

        def sgather(n):
            a, b, bank = PIECES[n]
            z = act([kv, ks, kn0], T.zs[:, a:b], R[4][:].indirect(T.nxu[:, 2 * M + a // 16:2 * M + b // 16]))
            return lambda: mm([z], B[bank][:, 0:b - a], idb, T.zs[:, a:b], False, True)

        def srelu(n, p):
            a, b, bank = PIECES[n]
            return act([p], T.qs[:, a:b], B[bank][:, 0:b - a], F.Relu, T.capf[:], -1.0)

        def base(x, p, q0):
            a0, b0, c0, c1, c2 = cols(x)
            act([p], T.x0[:, c0:c1], q0)
            return act([ksc], T.x0[:, c1:c2], q0, F.Identity, T.nsc[:], -1.0)

        def differ(x, deps2, q2, deps1, q1):
            a0, b0, c0, c1, c2 = cols(x)
            tt(deps2, o[:, c1:c2], T.x0[:, c1:c2], q2, A.subtract)
            k = tt(deps1, o[:, c0:c1], q1, T.x0[:, c0:c1], A.subtract)
            share([k], o[:, c0:c2], T["v%d_%d" % (rnd, rank)][:, c0:c2], "a%d_%d_%d" % (rnd, x, rank))
            return k

        preload([ks], PIECES[3:])
        h0a = vsum(0, 0, [kv, ks] + kd)
        h1a = vsum(1, 0, [])
        h0b = vsum(0, 1, [])
        z = [sgather(0)(), sgather(1)()]
        kre = [srelu(0, z[0]), srelu(1, z[1])]
        late = range(2, len(PIECES))
        p0a = fold([h0a, kzq, ul[3, 0]], B[0][:, 0:MA], T.zq, T.tv0, 0, SA)
        ppa = fold([kre[1], ul[3, 1]], B[1][:, MA:2 * MA], T.zq, T.qs, 0, SA)
        if OPT["z2"]:
            adds = [sgather(n) for n in late]
        kx = [base(0, p0a, B[0][:, 0:MA])]
        if not OPT["z2"]:
            adds = [sgather(n) for n in late]
        if OPT["add2"]:
            z = [f() for f in adds]
        p1a = fold([h1a], B[1][:, 0:MA], T.zq, T.qs, S + SB, 2 * S)
        if not OPT["add2"]:
            z = [f() for f in adds]
        kre += [srelu(n, z[n - 2]) for n in late]
        if OPT["sub"]:
            h1b = vsum(1, 1, [])
        ko = [differ(0, [kx[0], p1a], B[1][:, MA:2 * MA], [], B[1][:, 0:MA])]
        if not OPT["sub"]:
            h1b = vsum(1, 1, [])
        p0b = fold([h0b, ks], B[5][:, 0:MB], T.zq, T.tv0, SA, S)
        p1b = fold([h1b, kre[-1], ke, ul[0, 0]], B[6][:, 0:2 * MB], T.zq, T.qs, SA, S + SB)
        kx.append(base(1, p0b, B[5][:, 0:MB]))
        ko.append(differ(1, [kx[1], p1b], B[6][:, 0:MB], [], B[6][:, MB:2 * MB]))
        presum(0, [ke, kre[-1]])
        presum(1, [kx[0]])
        pD = [total(rnd, 0, ko[0])]
        if last:
            ky = tsc([kv, ks, tcap], T.yb[:], R[4][:], T.capf[:], None, A.min)
            wait("Y", ky, ("loc", sent[0]))
            sy = load("Y", "st0", T.yr[:], T.yb[:])
    for x in range(2):
        a, b, c0, c1, c2 = cols(x)
        kb = choose(x, pD[0] if x == 0 else total(ROUNDS - 1, 1, ko[1]))
        k = tt([kb], T.yf[:, a:b], T.bb[:, c0:c1], T.bb[:, c1:c2], A.add)
    wait("Y", k)
    sa = load("Y", "st1", T.ya[:], T.yf[:])
    wait("Y", sy, sa)
    wait("G", ("loc", sent[0]), ("cV", count["V"]), ("cS", count["S"]), ("cP", count["P"]), ("cG", count["G"]))
